import numpy as np
import ml_dtypes


def mxq(x, axis, fmt="e4m3"):
    dtype, down = {"e4m3": (ml_dtypes.float8_e4m3fn, 7), "e5m2": (ml_dtypes.float8_e5m2, 14)}[fmt]
    v = np.moveaxis(np.asarray(x, np.float32).astype(ml_dtypes.bfloat16).astype(np.float64), axis, -1)
    blocks = v.reshape(v.shape[:-1] + (-1, 32))
    amax = np.abs(blocks).max(-1, keepdims=True)
    byte = np.maximum(np.where(amax > 0, np.frexp(amax)[1] - 1 + 127, 0) - down, 1)
    scale = np.exp2(byte - 127.0)
    codes = (blocks / scale).astype(np.float32).astype(dtype).astype(np.float64)
    return np.moveaxis((codes * scale).reshape(v.shape), -1, axis)


WIDE = False


def mx_kscale(k):
    if not WIDE:
        return np.ones(k)
    levels = np.array([24, -24, 12, -12, 0])
    if k % 512:
        return np.exp2(np.random.permutation(np.resize(levels, k // 32))).repeat(32)
    a = np.empty((k // 512, 16))
    for p in range(k // 512):
        a[p, :8] = np.random.permutation(np.resize(levels, 8))
        for g in range(8):
            far = levels[np.abs(levels - a[p, g]) >= 10]
            a[p, g + 8] = far[np.random.randint(len(far))]
    return np.exp2(a.ravel()).repeat(32)


def f64(x):
    return np.asarray(x).astype(np.float64)


def striped(idx):
    return np.tile(idx.reshape(-1, 16).T, (8, 1)).astype(np.uint16)


def unstriped(offs):
    return offs[:16].T.reshape(-1).astype(np.int64)


def striped8(idx):
    return np.concatenate([v.reshape(-1, 16).T for v in idx]).astype(np.uint16)


def unstriped8(offs):
    return np.stack([offs[16 * g:16 * g + 16].T.reshape(-1) for g in range(8)]).astype(np.int64)


E2M1 = np.array([0.0, 0.5, 1.0, 1.5, 2.0, 3.0, 4.0, 6.0, -0.0, -0.5, -1.0, -1.5, -2.0, -3.0, -4.0, -6.0])


def pack_weight(w, fmt):
    k, n = w.shape
    w = f64(np.asarray(w, np.float32).astype(ml_dtypes.bfloat16)).reshape(k // 32, 32, n)
    amax = np.abs(w).max(1)
    if fmt == "e4m3":
        byte = np.frexp(amax)[1] - 1 + 127 - 7
    else:
        mant, ex = np.frexp(amax / 6.0)
        byte = np.where(mant > 0.5, ex, ex - 1) + 127
    byte = np.clip(np.where(amax > 0, byte, 1), 1, 254)
    scaled = (w * np.exp2(127.0 - byte)[:, None, :]).reshape(k, n).astype(np.float32)
    by_word = np.ascontiguousarray(scaled.reshape(k // 512, 128, 4, n).transpose(0, 1, 3, 2))
    if fmt == "e4m3":
        words = by_word.astype(ml_dtypes.float8_e4m3fn).view(np.uint8)
    else:
        c = by_word.astype(ml_dtypes.float4_e2m1fn).view(np.uint8) & 0xF
        words = (c[..., 0::2] | (c[..., 1::2] << 4)).reshape(k // 512, 128, 2 * n)
    return np.ascontiguousarray(words), np.ascontiguousarray(byte.astype(np.uint8).reshape(k // 512, 16, n))


def unpack_weight(words, scales, fmt):
    g, _, n = scales.shape
    words = np.ascontiguousarray(words).reshape(g, 128, n, -1)
    if fmt == "e4m3":
        vals = words.view(ml_dtypes.float8_e4m3fn).astype(np.float64)
    else:
        nib = np.empty((g, 128, n, 4), np.uint8)
        nib[..., 0::2] = words & 0xF
        nib[..., 1::2] = words >> 4
        vals = E2M1[nib]
    vals = vals * np.repeat(np.exp2(scales.astype(np.float64) - 127.0), 8, axis=1)[..., None]
    return vals.transpose(0, 1, 3, 2).reshape(g * 512, n)


def pack_table4(v):
    words, scales = pack_weight(v, "e2m1")
    g, t = words.shape[0] // 2, v.shape[1]
    return np.ascontiguousarray(words.reshape(g, 2, 128, t, 2).transpose(0, 2, 3, 1, 4).reshape(g, 128, t, 4)), scales


def unpack_table4(words, scales):
    g, _, t, _ = words.shape
    return unpack_weight(words.reshape(g, 128, t, 2, 2).transpose(0, 3, 1, 2, 4).reshape(2 * g, 128, 2 * t), scales, "e2m1")


def planes(y):
    n, m = y.shape
    v = y.astype(np.float32).astype(ml_dtypes.bfloat16).astype(np.float64).reshape(n // 32, 32, m)
    top = np.abs(v).max(1)
    byte = np.clip(np.where(top > 0, np.frexp(top)[1] - 1 + 127 - 7, 1), 1, 254)
    codes = (v * np.exp2(127.0 - byte)[:, None, :]).reshape(n, m).astype(np.float32).astype(ml_dtypes.float8_e4m3fn).view(np.uint8)
    words = codes.reshape(n // 512, 128, 4, m).transpose(0, 1, 3, 2)
    return np.ascontiguousarray(words), np.ascontiguousarray(byte.astype(np.uint8).reshape(n // 512, 16, m))


def silu(f):
    return f / (1.0 + np.exp(-np.maximum(f, -700.0)))


K, L, R, N, T, J = 512, 1024, 512, 512, 2048, 1024


def setup_inputs():
    n = np.random.standard_normal
    s = mx_kscale(K)[:, None]
    s2 = mx_kscale(L)[:, None]
    u = mx_kscale(R)[:, None]
    p_tab = pack_table4(n((L, T)) * s2)
    p_wb = pack_weight(n((L, R)) / np.sqrt(L) / s2 * u.T, "e2m1")
    p_wd = pack_weight(n((R, N)) / np.sqrt(R) / u, "e4m3")
    return {
        "tab_words": p_tab[0],
        "tab_scales": p_tab[1],
        "xT": (n((K, T)) * s).astype(np.float32),
        "wgt2": np.repeat(np.random.uniform(0.5, 2.0, (8, J)), 16, axis=0).astype(np.float32),
        "wa": (n((K, R)) / np.sqrt(K) / s).astype(np.float32),
        "wb_words": p_wb[0],
        "wb_scales": p_wb[1],
        "wd_words": p_wd[0],
        "wd_scales": p_wd[1],
        "b": (0.3 * n(N)).astype(np.float32),
        "offs": striped(np.random.permutation(T)[:J]),
        "offs2": striped8(np.stack([np.random.permutation(T)[:J] for _ in range(8)])),
    }


def reference(tab_words, tab_scales, xT, wgt2, wa, wb_words, wb_scales, wd_words, wd_scales, b, offs, offs2):
    idx = unstriped(offs)
    idx2 = unstriped8(offs2)
    tab_ = unpack_table4(tab_words, tab_scales)[:, idx]
    rows = np.arange(K)
    xg = f64(wgt2)[rows // 4 % 128] * f64(xT)[rows[:, None], idx2[rows % 512 // 64]]
    xT_ = mxq(xg, 0, "e4m3")
    wa_ = mxq(f64(wa), 0, "e4m3")
    wb_ = unpack_weight(wb_words, wb_scales, "e2m1")
    ya = wa_.T @ xT_
    yb = wb_.T @ tab_
    h = silu(ya) * yb
    h_ = mxq(h, 0, "e4m3")
    wd_ = unpack_weight(wd_words, wd_scales, "e4m3")
    y = wd_.T @ h_
    out_0 = y + f64(b)[:, None]
    return (out_0,) + planes(out_0)

@@ -1,0 +1,237 @@
+from contextlib import ExitStack
+
+import concourse.mybir as mybir
+
+K, L, R, N, T, J = 512, 1024, 512, 512, 2048, 1024
+FLOPS = 2 * J * (K * R + L * R + R * N)
+
+F32 = mybir.dt.float32
+BF16 = mybir.dt.bfloat16
+I32 = mybir.dt.int32
+U32 = mybir.dt.uint32
+U16 = mybir.dt.uint16
+U8 = mybir.dt.uint8
+FP8X4 = mybir.dt.float8_e4m3fn_x4
+FP4X4 = mybir.dt.float4_e2m1fn_x4
+ACT = mybir.ActivationFunctionType
+MULT = mybir.AluOpType.mult
+
+P = 128
+PACK = 4
+SUB = 128
+WIDTHS = (256, 256, 256, 128, 128)
+STARTS = (0, 256, 512, 768, 896)
+NCH = len(WIDTHS)
+HALF = J // 2
+
+
+def tile_list_htabg_glu_biasP_kernel(
+    tc, tab_words, tab_scales, xT, wgt2, wa, wb_words, wb_scales, wd_words, wd_scales, b, offs, offs2,
+    out_0, out_1, out_2,
+):
+    nc = tc.nc
+    with ExitStack() as ctx:
+        lists = ctx.enter_context(tc.tile_pool(name="lists", bufs=1))
+        keep = ctx.enter_context(tc.tile_pool(name="keep", bufs=1))
+        ring = ctx.enter_context(tc.tile_pool(name="ring", bufs=NCH))
+        psum = ctx.enter_context(tc.psum_pool(name="psum", bufs=8))
+
+        idx = lists.tile([P, J // 16], U16)
+        idx2 = lists.tile([P, J // 16], U16)
+        tab_w = keep.tile([P, T], I32, align_bytes=64)
+        tab_s = keep.tile([P, T], U8, align_bytes=64)
+        got_s = keep.tile([P, J], U8, align_bytes=64)
+        got_s1 = keep.tile([P, J], U8, align_bytes=64)
+        planes = [keep.tile([P, T], F32, name="x_plane%d" % i, align_bytes=64) for i in range(PACK)]
+        wgt = keep.tile([P, J], F32, align_bytes=64)
+        wa_raw = keep.tile([P, PACK, R], F32, align_bytes=64)
+        wa_bf = keep.tile([P, R * PACK], BF16, align_bytes=64)
+        wa_q = keep.tile([P, R], U32, align_bytes=64)
+        wa_s = keep.tile([P, R], U8, align_bytes=64)
+        wb_raw = keep.tile([P, 2, 2 * R], U8, align_bytes=64)
+        wb_q = keep.tile([P, 2, 2 * R], U8, align_bytes=64)
+        wd_raw = keep.tile([P, N], I32, align_bytes=64)
+        wd_q = keep.tile([P, N], I32, align_bytes=64)
+        ws_raw = keep.tile([P, 2, R], U8, align_bytes=64)
+        ws = keep.tile([P, 2, R], U8, align_bytes=64)
+        ds_raw = keep.tile([P, N], U8, align_bytes=64)
+        ds = keep.tile([P, N], U8, align_bytes=64)
+        bias = keep.tile([P, PACK], F32, align_bytes=64)
+        out_s = keep.tile([P, J], U8, align_bytes=64)
+        zero = keep.tile([P, 1], F32, align_bytes=64)
+        warm = keep.tile([P, 1], F32, align_bytes=64)
+
+        nc.gpsimd.memset(tab_s[:].bitcast(I32), 0)
+        nc.vector.memset(zero[:], 0.0)
+        nc.scalar.activation(warm[:], zero[:], ACT.Silu)
+        nc.gpsimd.memset(ws_raw[:].rearrange("p a r -> p (a r)").bitcast(I32), 0)
+        nc.gpsimd.memset(ds_raw[:].bitcast(I32), 0)
+        nc.gpsimd.memset(got_s1[:].bitcast(I32), 0)
+
+        x_rows = xT.rearrange("(p i) t -> i p t", i=PACK)
+        nc.sync.dma_start(wb_raw[:].bitcast(I32), wb_words.rearrange("a p c -> p a c").bitcast(I32))
+        nc.sync.dma_start(idx[:], offs)
+        for q in range(4):
+            nc.sync.dma_start(tab_s[32 * q : 32 * q + 8, :].bitcast(I32), tab_scales[:, 4 * q : 4 * q + 4, :].bitcast(I32))
+        nc.sync.dma_start(tab_w[:], tab_words[0].rearrange("p t b -> p (t b)").bitcast(I32))
+        nc.sync.dma_start(wa_raw[:], wa.rearrange("(p i) r -> p i r", i=PACK))
+        nc.sync.dma_start(idx2[:], offs2)
+        nc.sync.dma_start(wgt[:], wgt2)
+        nc.sync.dma_start(planes[0][:], x_rows[0])
+        for q in range(4):
+            nc.sync.dma_start(
+                ws_raw[32 * q : 32 * q + 4, :, :].bitcast(I32),
+                wb_scales[:, 4 * q : 4 * q + 4, :].rearrange("a r c -> r a c").bitcast(I32),
+            )
+        nc.sync.dma_start(planes[1][:], x_rows[1])
+        nc.sync.dma_start(planes[2][:], x_rows[2])
+        for q in range(4):
+            nc.sync.dma_start(
+                ds_raw[32 * q : 32 * q + 4, :].bitcast(I32), wd_scales[0, 4 * q : 4 * q + 4, :].bitcast(I32)
+            )
+        nc.sync.dma_start(planes[3][:], x_rows[3])
+        nc.sync.dma_start(wd_raw[:], wd_words[0].rearrange("p n b -> p (n b)").bitcast(I32))
+        nc.sync.dma_start(bias[:], b.rearrange("(p t) -> p t", t=PACK))
+
+        nc.vector.tensor_copy(
+            wb_q[:].bitcast(U16).rearrange("p a (t m) -> p a m t", t=PACK),
+            wb_raw[:].bitcast(U16).rearrange("p a (m t) -> p a m t", t=PACK),
+        )
+        nc.vector.tensor_copy(got_s[:], tab_s[:].indirect(idx[:]))
+        nc.scalar.dma_start(got_s1[0:100, :].bitcast(I32), got_s[4:104, :].bitcast(I32))
+
+        picked = [ring.tile([P, PACK, w], F32, name="picked") for w in WIDTHS]
+        x_q = [ring.tile([P, w], U32, name="x_q", align_bytes=64) for w in WIDTHS]
+        x_s = [ring.tile([P, w], U8, name="x_s", align_bytes=64) for w in WIDTHS]
+        x_bf = [ring.tile([P, w, PACK], BF16, name="x_bf", align_bytes=64) for w in WIDTHS]
+        t_q = [keep.tile([P, 2, 2 * HALF], U8, name="t_q%d" % u, align_bytes=64) for u in range(2)]
+        got_w = [keep.tile([P, HALF], U32, name="got_w%d" % u, align_bytes=64) for u in range(2)]
+        h_bf = [ring.tile([P, w, PACK], BF16, name="h_bf", align_bytes=64) for w in WIDTHS]
+        act = [ring.tile([P, w, PACK], F32, name="act", align_bytes=64) for w in WIDTHS]
+        yb_sb = [ring.tile([P, w, PACK], F32, name="yb_sb", align_bytes=64) for w in WIDTHS]
+        y_sb = [ring.tile([P, PACK, w], F32, name="y_sb", align_bytes=64) for w in WIDTHS]
+        y_bf = [ring.tile([P, w, PACK], BF16, name="y_bf", align_bytes=64) for w in WIDTHS]
+
+        def cols(c):
+            return slice(STARTS[c], STARTS[c] + WIDTHS[c])
+
+        def entries(lst, j0, n):
+            return lst[:, j0 // 16 : (j0 + n) // 16]
+
+        def interleave(copy, dst, src):
+            copy(dst.rearrange("p (c i) t -> p c t i", i=4), src.rearrange("p t (c i) -> p c t i", i=4))
+
+        def quantize(codes, scales, src):
+            nc.vector.quantize_mx(out=codes.bitcast(FP8X4), scales=scales, in_=src)
+
+        def pick_x(c, i):
+            nc.vector.tensor_tensor(picked[c][:, i, :], planes[i][:].indirect(entries(idx2, STARTS[c], WIDTHS[c])), wgt[:, cols(c)], MULT)
+
+        def round_x(c):
+            interleave(nc.scalar.copy if c < 3 else nc.vector.tensor_copy, x_bf[c][:], picked[c][:])
+
+        def quant_x(c):
+            quantize(x_q[c][:], x_s[c][:], x_bf[c][:].rearrange("p c t -> p (c t)"))
+
+        def pick_tab(u):
+            nc.vector.tensor_copy(got_w[u][:], tab_w[:].bitcast(U32).indirect(entries(idx, u * HALF, HALF)))
+
+        def part_tab(u):
+            nc.vector.tensor_copy(t_q[u][:].bitcast(U16), got_w[u][:].bitcast(U16).rearrange("p (j d) -> p d j", d=2))
+
+        def memory(c, s):
+            yb = psum.tile([P, PACK, SUB], F32, name="bank")
+            j0 = STARTS[c] + s * SUB
+            jh = j0 % HALF
+            for t in range(PACK):
+                for a in range(2):
+                    nc.tensor.matmul_mx(
+                        out=yb[:, t, :], lhsT=wb_q[:, a, 2 * t * P : 2 * (t + 1) * P].bitcast(FP4X4),
+                        lhsT_scale=ws[:, a, t * P : (t + 1) * P],
+                        rhs=t_q[j0 // HALF][:, a, 2 * jh : 2 * (jh + SUB)].bitcast(FP4X4),
+                        rhs_scale=(got_s, got_s1)[a][:, j0 : j0 + SUB], start=(a == 0), stop=(a == 1),
+                    )
+            nc.scalar.copy(yb_sb[c][:, s * SUB : (s + 1) * SUB, :], yb[:].rearrange("p t n -> p n t"))
+
+        def gate(c, s):
+            sub = slice(s * SUB, (s + 1) * SUB)
+            ya = psum.tile([P, PACK, SUB], F32, name="bank")
+            for t in range(PACK):
+                m = slice(t * P, (t + 1) * P)
+                nc.tensor.matmul_mx(
+                    out=ya[:, t, :], lhsT=wa_q[:, m].bitcast(FP8X4), lhsT_scale=wa_s[:, m],
+                    rhs=x_q[c][:, sub].bitcast(FP8X4), rhs_scale=x_s[c][:, sub], start=True, stop=True,
+                )
+            nc.scalar.activation(act[c][:, sub, :], ya[:].rearrange("p t n -> p n t"), ACT.Silu)
+
+        def join(c):
+            nc.vector.tensor_tensor(h_bf[c][:], act[c][:], yb_sb[c][:], MULT)
+
+        def down(c):
+            w = WIDTHS[c]
+            per_bank = 512 // w
+            h_q = ring.tile([P, w], U32, name="h_q", align_bytes=64)
+            h_s = ring.tile([P, w], U8, name="h_s", align_bytes=64)
+            quantize(h_q[:], h_s[:], h_bf[c][:].rearrange("p c t -> p (c t)"))
+            for t0 in range(0, PACK, per_bank):
+                y = psum.tile([P, per_bank, w], F32, name="bank")
+                for e in range(per_bank):
+                    m = slice((t0 + e) * P, (t0 + e + 1) * P)
+                    nc.tensor.matmul_mx(
+                        out=y[:, e, :], lhsT=wd_q[:, m].bitcast(FP8X4), lhsT_scale=ds[:, m],
+                        rhs=h_q[:].bitcast(FP8X4), rhs_scale=h_s[:], start=True, stop=True,
+                    )
+                for e in range(per_bank):
+                    t = t0 + e
+                    nc.scalar.activation(y_sb[c][:, t, :], y[:, e, :], ACT.Identity, bias=bias[:, t : t + 1])
+            nc.sync.dma_start(out_0.rearrange("(p t) j -> p t j", t=PACK)[:, :, cols(c)], y_sb[c][:])
+
+        def round_y(c):
+            interleave(nc.vector.tensor_copy, y_bf[c][:], y_sb[c][:])
+
+        def emit(c):
+            y_q = ring.tile([P, WIDTHS[c]], I32, name="y_q", align_bytes=64)
+            quantize(y_q[:], out_s[:, cols(c)], y_bf[c][:].rearrange("p c t -> p (c t)"))
+            nc.sync.dma_start(out_1[0].rearrange("p j b -> p (j b)").bitcast(I32)[:, cols(c)], y_q[:])
+
+        for u in range(2):
+            pick_tab(u)
+        for u in range(2):
+            part_tab(u)
+        nc.vector.tensor_copy(
+            ws[:].rearrange("p a (t m) -> p a m t", t=PACK), ws_raw[:].rearrange("p a (m t) -> p a m t", t=PACK)
+        )
+        nc.scalar.copy(
+            wa_bf[:].rearrange("p (t m i) -> p m t i", t=PACK, i=PACK),
+            wa_raw[:].rearrange("p i (m t) -> p m t i", t=PACK),
+        )
+        quantize(wa_q[:], wa_s[:], wa_bf[:])
+        for c in range(NCH):
+            for s in range(WIDTHS[c] // SUB):
+                memory(c, s)
+        for i in range(PACK - 1):
+            for c in range(NCH):
+                pick_x(c, i)
+        nc.vector.tensor_copy(ds[:].rearrange("p (t m) -> p m t", t=PACK), ds_raw[:].rearrange("p (m t) -> p m t", t=PACK))
+        for c in range(NCH):
+            pick_x(c, PACK - 1)
+            round_x(c)
+        nc.vector.tensor_copy(
+            wd_q[:].rearrange("p (t m) -> p m t", t=PACK), wd_raw[:].rearrange("p (m t) -> p m t", t=PACK)
+        )
+        for step in range(NCH + 4):
+            if step < NCH:
+                quant_x(step)
+                for s in range(WIDTHS[step] // SUB):
+                    gate(step, s)
+            if 0 <= step - 4 < NCH:
+                emit(step - 4)
+            if 0 <= step - 1 < NCH:
+                join(step - 1)
+            if 0 <= step - 3 < NCH:
+                round_y(step - 3)
+            if 0 <= step - 2 < NCH:
+                down(step - 2)
+        for q in range(4):
+            queue = nc.scalar if q % 2 else nc.sync
+            queue.dma_start(out_2[0, 4 * q : 4 * q + 4, :].bitcast(I32), out_s[32 * q : 32 * q + 4, :].bitcast(I32))

@@ -23,6 +23,8 @@ WIDTHS = (256, 256, 256, 128, 128)
 STARTS = (0, 256, 512, 768, 896)
 NCH = len(WIDTHS)
 HALF = J // 2
+CH = 256
+NG = J // CH
 
 
 def tile_list_htabg_glu_biasP_kernel(
@@ -46,6 +48,7 @@ def tile_list_htabg_glu_biasP_kernel(
         wgt = keep.tile([P, J], F32, align_bytes=64)
         wa_raw = keep.tile([P, PACK, R], F32, align_bytes=64)
         wa_bf = keep.tile([P, R * PACK], BF16, align_bytes=64)
+        wa_nat = keep.tile([P, R, PACK], BF16, align_bytes=64)
         wa_q = keep.tile([P, R], U32, align_bytes=64)
         wa_s = keep.tile([P, R], U8, align_bytes=64)
         wb_raw = keep.tile([P, 2, 2 * R], U8, align_bytes=64)
@@ -69,43 +72,43 @@ def tile_list_htabg_glu_biasP_kernel(
         nc.gpsimd.memset(got_s1[:].bitcast(I32), 0)
 
         x_rows = xT.rearrange("(p i) t -> i p t", i=PACK)
-        nc.sync.dma_start(wb_raw[:].bitcast(I32), wb_words.rearrange("a p c -> p a c").bitcast(I32))
         nc.sync.dma_start(idx[:], offs)
+        nc.sync.dma_start(wb_raw[:].bitcast(I32), wb_words.rearrange("a p c -> p a c").bitcast(I32))
         for q in range(4):
             nc.sync.dma_start(tab_s[32 * q : 32 * q + 8, :].bitcast(I32), tab_scales[:, 4 * q : 4 * q + 4, :].bitcast(I32))
         nc.sync.dma_start(tab_w[:], tab_words[0].rearrange("p t b -> p (t b)").bitcast(I32))
         nc.sync.dma_start(wa_raw[:], wa.rearrange("(p i) r -> p i r", i=PACK))
-        nc.sync.dma_start(idx2[:], offs2)
-        nc.sync.dma_start(wgt[:], wgt2)
-        nc.sync.dma_start(planes[0][:], x_rows[0])
         for q in range(4):
             nc.sync.dma_start(
                 ws_raw[32 * q : 32 * q + 4, :, :].bitcast(I32),
                 wb_scales[:, 4 * q : 4 * q + 4, :].rearrange("a r c -> r a c").bitcast(I32),
             )
+        nc.sync.dma_start(idx2[:], offs2)
+        nc.sync.dma_start(wgt[:], wgt2)
+        nc.sync.dma_start(planes[0][:], x_rows[0])
         nc.sync.dma_start(planes[1][:], x_rows[1])
-        nc.sync.dma_start(planes[2][:], x_rows[2])
         for q in range(4):
             nc.sync.dma_start(
                 ds_raw[32 * q : 32 * q + 4, :].bitcast(I32), wd_scales[0, 4 * q : 4 * q + 4, :].bitcast(I32)
             )
+        nc.sync.dma_start(planes[2][:], x_rows[2])
         nc.sync.dma_start(planes[3][:], x_rows[3])
         nc.sync.dma_start(wd_raw[:], wd_words[0].rearrange("p n b -> p (n b)").bitcast(I32))
         nc.sync.dma_start(bias[:], b.rearrange("(p t) -> p t", t=PACK))
 
         nc.vector.tensor_copy(
-            wb_q[:].bitcast(U16).rearrange("p a (t m) -> p a m t", t=PACK),
-            wb_raw[:].bitcast(U16).rearrange("p a (m t) -> p a m t", t=PACK),
+            wb_q[:].bitcast(U16).rearrange("p a (t m) -> p a t m", t=PACK),
+            wb_raw[:].bitcast(U16).rearrange("p a (m t) -> p a t m", t=PACK),
         )
         nc.vector.tensor_copy(got_s[:], tab_s[:].indirect(idx[:]))
         nc.scalar.dma_start(got_s1[0:100, :].bitcast(I32), got_s[4:104, :].bitcast(I32))
 
-        picked = [ring.tile([P, PACK, w], F32, name="picked") for w in WIDTHS]
-        x_q = [ring.tile([P, w], U32, name="x_q", align_bytes=64) for w in WIDTHS]
-        x_s = [ring.tile([P, w], U8, name="x_s", align_bytes=64) for w in WIDTHS]
-        x_bf = [ring.tile([P, w, PACK], BF16, name="x_bf", align_bytes=64) for w in WIDTHS]
+        early = keep.tile([P, PACK, 3 * CH], F32, align_bytes=64)
+        x_q = [ring.tile([P, CH], U32, name="x_q", align_bytes=64) for g in range(NG)]
+        x_s = [ring.tile([P, CH], U8, name="x_s", align_bytes=64) for g in range(NG)]
+        x_bf = [ring.tile([P, CH, PACK], BF16, name="x_bf", align_bytes=64) for g in range(NG)]
         t_q = [keep.tile([P, 2, 2 * HALF], U8, name="t_q%d" % u, align_bytes=64) for u in range(2)]
-        got_w = [keep.tile([P, HALF], U32, name="got_w%d" % u, align_bytes=64) for u in range(2)]
+        got_w = keep.tile([P, J], U32, align_bytes=64)
         h_bf = [ring.tile([P, w, PACK], BF16, name="h_bf", align_bytes=64) for w in WIDTHS]
         act = [ring.tile([P, w, PACK], F32, name="act", align_bytes=64) for w in WIDTHS]
         yb_sb = [ring.tile([P, w, PACK], F32, name="yb_sb", align_bytes=64) for w in WIDTHS]
@@ -124,20 +127,29 @@ def tile_list_htabg_glu_biasP_kernel(
         def quantize(codes, scales, src):
             nc.vector.quantize_mx(out=codes.bitcast(FP8X4), scales=scales, in_=src)
 
-        def pick_x(c, i):
-            nc.vector.tensor_tensor(picked[c][:, i, :], planes[i][:].indirect(entries(idx2, STARTS[c], WIDTHS[c])), wgt[:, cols(c)], MULT)
+        def pick_x(dst, i, j0, n):
+            nc.vector.tensor_tensor(dst, planes[i][:].indirect(entries(idx2, j0, n)), wgt[:, j0 : j0 + n], MULT)
 
-        def round_x(c):
-            interleave(nc.scalar.copy if c < 3 else nc.vector.tensor_copy, x_bf[c][:], picked[c][:])
+        def picked(g):
+            return early[:, :, g % 3 * CH : (g % 3 + 1) * CH]
 
-        def quant_x(c):
-            quantize(x_q[c][:], x_s[c][:], x_bf[c][:].rearrange("p c t -> p (c t)"))
+        def pick_last(g):
+            pick_x(early[:, PACK - 1, g * CH : (g + 1) * CH], PACK - 1, g * CH, CH)
 
-        def pick_tab(u):
-            nc.vector.tensor_copy(got_w[u][:], tab_w[:].bitcast(U32).indirect(entries(idx, u * HALF, HALF)))
+        def pick_late(i):
+            pick_x(early[:, i, 0:CH], i, 3 * CH, CH)
+
+        def round_x(g):
+            interleave(nc.scalar.copy, x_bf[g][:], picked(g))
+
+        def quant_x(g):
+            quantize(x_q[g][:], x_s[g][:], x_bf[g][:].rearrange("p c t -> p (c t)"))
 
         def part_tab(u):
-            nc.vector.tensor_copy(t_q[u][:].bitcast(U16), got_w[u][:].bitcast(U16).rearrange("p (j d) -> p d j", d=2))
+            nc.vector.tensor_copy(
+                t_q[u][:].bitcast(U16),
+                got_w[:, u * HALF : (u + 1) * HALF].bitcast(U16).rearrange("p (j d) -> p d j", d=2),
+            )
 
         def memory(c, s):
             yb = psum.tile([P, PACK, SUB], F32, name="bank")
@@ -153,16 +165,18 @@ def tile_list_htabg_glu_biasP_kernel(
                     )
             nc.scalar.copy(yb_sb[c][:, s * SUB : (s + 1) * SUB, :], yb[:].rearrange("p t n -> p n t"))
 
-        def gate(c, s):
-            sub = slice(s * SUB, (s + 1) * SUB)
-            ya = psum.tile([P, PACK, SUB], F32, name="bank")
-            for t in range(PACK):
-                m = slice(t * P, (t + 1) * P)
-                nc.tensor.matmul_mx(
-                    out=ya[:, t, :], lhsT=wa_q[:, m].bitcast(FP8X4), lhsT_scale=wa_s[:, m],
-                    rhs=x_q[c][:, sub].bitcast(FP8X4), rhs_scale=x_s[c][:, sub], start=True, stop=True,
-                )
-            nc.scalar.activation(act[c][:, sub, :], ya[:].rearrange("p t n -> p n t"), ACT.Silu)
+        def gate(g):
+            for s in range(CH // SUB):
+                sub = slice(s * SUB, (s + 1) * SUB)
+                ya = psum.tile([P, PACK, SUB], F32, name="bank")
+                for t in range(PACK):
+                    m = slice(t * P, (t + 1) * P)
+                    nc.tensor.matmul_mx(
+                        out=ya[:, t, :], lhsT=wa_q[:, m].bitcast(FP8X4), lhsT_scale=wa_s[:, m],
+                        rhs=x_q[g][:, sub].bitcast(FP8X4), rhs_scale=x_s[g][:, sub], start=True, stop=True,
+                    )
+                dst = act[g][:, sub, :] if g < 3 else act[3 + s][:]
+                nc.scalar.activation(dst, ya[:].rearrange("p t n -> p n t"), ACT.Silu)
 
         def join(c):
             nc.vector.tensor_tensor(h_bf[c][:], act[c][:], yb_sb[c][:], MULT)
@@ -194,44 +208,64 @@ def tile_list_htabg_glu_biasP_kernel(
             quantize(y_q[:], out_s[:, cols(c)], y_bf[c][:].rearrange("p c t -> p (c t)"))
             nc.sync.dma_start(out_1[0].rearrange("p j b -> p (j b)").bitcast(I32)[:, cols(c)], y_q[:])
 
-        for u in range(2):
-            pick_tab(u)
+        nc.vector.tensor_copy(got_w[:], tab_w[:].bitcast(U32).indirect(idx[:]))
         for u in range(2):
             part_tab(u)
         nc.vector.tensor_copy(
-            ws[:].rearrange("p a (t m) -> p a m t", t=PACK), ws_raw[:].rearrange("p a (m t) -> p a m t", t=PACK)
+            ws[:].rearrange("p a (t m) -> p a t m", t=PACK), ws_raw[:].rearrange("p a (m t) -> p a t m", t=PACK)
         )
+        interleave(nc.scalar.copy, wa_nat[:], wa_raw[:])
         nc.scalar.copy(
-            wa_bf[:].rearrange("p (t m i) -> p m t i", t=PACK, i=PACK),
-            wa_raw[:].rearrange("p i (m t) -> p m t i", t=PACK),
+            wa_bf[:].bitcast(F32).rearrange("p (t m e) -> p t m e", t=PACK, e=2),
+            wa_nat[:].rearrange("p r i -> p (r i)").bitcast(F32).rearrange("p (m t e) -> p t m e", t=PACK, e=2),
         )
         quantize(wa_q[:], wa_s[:], wa_bf[:])
         for c in range(NCH):
             for s in range(WIDTHS[c] // SUB):
                 memory(c, s)
         for i in range(PACK - 1):
-            for c in range(NCH):
-                pick_x(c, i)
-        nc.vector.tensor_copy(ds[:].rearrange("p (t m) -> p m t", t=PACK), ds_raw[:].rearrange("p (m t) -> p m t", t=PACK))
-        for c in range(NCH):
-            pick_x(c, PACK - 1)
-            round_x(c)
+            pick_x(early[:, i, :], i, 0, 3 * CH)
+        nc.vector.tensor_copy(ds[:].rearrange("p (t m) -> p t m", t=PACK), ds_raw[:].rearrange("p (m t) -> p t m", t=PACK))
+        pick_last(0)
+        round_x(0)
+        pick_last(1)
+        round_x(1)
         nc.vector.tensor_copy(
-            wd_q[:].rearrange("p (t m) -> p m t", t=PACK), wd_raw[:].rearrange("p (m t) -> p m t", t=PACK)
+            wd_q[:].rearrange("p (t m i) -> p m t i", t=PACK, i=4), wd_raw[:].rearrange("p (m i t) -> p m t i", t=PACK, i=4)
         )
-        for step in range(NCH + 4):
-            if step < NCH:
-                quant_x(step)
-                for s in range(WIDTHS[step] // SUB):
-                    gate(step, s)
-            if 0 <= step - 4 < NCH:
-                emit(step - 4)
-            if 0 <= step - 1 < NCH:
-                join(step - 1)
-            if 0 <= step - 3 < NCH:
-                round_y(step - 3)
-            if 0 <= step - 2 < NCH:
-                down(step - 2)
+        pick_last(2)
+        round_x(2)
+        quant_x(0)
+        gate(0)
+        pick_late(0)
+        pick_late(1)
+        quant_x(1)
+        gate(1)
+        pick_late(2)
+        pick_late(3)
+        round_x(3)
+        quant_x(2)
+        join(0)
+        gate(2)
+        down(0)
+        join(1)
+        quant_x(3)
+        gate(3)
+        down(1)
+        join(2)
+        round_y(0)
+        down(2)
+        join(3)
+        emit(0)
+        join(4)
+        down(3)
+        round_y(1)
+        down(4)
+        emit(1)
+        for c in range(2, NCH):
+            round_y(c)
+        for c in range(2, NCH):
+            emit(c)
         for q in range(4):
             queue = nc.scalar if q % 2 else nc.sync
             queue.dma_start(out_2[0, 4 * q : 4 * q + 4, :].bitcast(I32), out_s[32 * q : 32 * q + 4, :].bitcast(I32))

@@ -60,9 +60,9 @@ def tile_list_htabg_glu_biasP_kernel(
         ds_raw = keep.tile([P, N], U8, align_bytes=64)
         ds = keep.tile([P, N], U8, align_bytes=64)
         bias = keep.tile([P, PACK], F32, align_bytes=64)
-        out_s = keep.tile([P, J], U8, align_bytes=64)
         zero = keep.tile([P, 1], F32, align_bytes=64)
         warm = keep.tile([P, 1], F32, align_bytes=64)
+        out_s = keep.tile([P, J], U8, align_bytes=64)
 
         nc.gpsimd.memset(tab_s[:].bitcast(I32), 0)
         nc.vector.memset(zero[:], 0.0)
@@ -87,12 +87,12 @@ def tile_list_htabg_glu_biasP_kernel(
         nc.sync.dma_start(wgt[:], wgt2)
         nc.sync.dma_start(planes[0][:], x_rows[0])
         nc.sync.dma_start(planes[1][:], x_rows[1])
+        nc.sync.dma_start(planes[2][:], x_rows[2])
+        nc.sync.dma_start(planes[3][:], x_rows[3])
         for q in range(4):
             nc.sync.dma_start(
                 ds_raw[32 * q : 32 * q + 4, :].bitcast(I32), wd_scales[0, 4 * q : 4 * q + 4, :].bitcast(I32)
             )
-        nc.sync.dma_start(planes[2][:], x_rows[2])
-        nc.sync.dma_start(planes[3][:], x_rows[3])
         nc.sync.dma_start(wd_raw[:], wd_words[0].rearrange("p n b -> p (n b)").bitcast(I32))
         nc.sync.dma_start(bias[:], b.rearrange("(p t) -> p t", t=PACK))
 
@@ -103,7 +103,7 @@ def tile_list_htabg_glu_biasP_kernel(
         nc.vector.tensor_copy(got_s[:], tab_s[:].indirect(idx[:]))
         nc.scalar.dma_start(got_s1[0:100, :].bitcast(I32), got_s[4:104, :].bitcast(I32))
 
-        early = keep.tile([P, PACK, 3 * CH], F32, align_bytes=64)
+        early = keep.tile([P, PACK, J], F32, align_bytes=64)
         x_q = [ring.tile([P, CH], U32, name="x_q", align_bytes=64) for g in range(NG)]
         x_s = [ring.tile([P, CH], U8, name="x_s", align_bytes=64) for g in range(NG)]
         x_bf = [ring.tile([P, CH, PACK], BF16, name="x_bf", align_bytes=64) for g in range(NG)]
@@ -131,16 +131,13 @@ def tile_list_htabg_glu_biasP_kernel(
             nc.vector.tensor_tensor(dst, planes[i][:].indirect(entries(idx2, j0, n)), wgt[:, j0 : j0 + n], MULT)
 
         def picked(g):
-            return early[:, :, g % 3 * CH : (g % 3 + 1) * CH]
+            return early[:, :, g * CH : (g + 1) * CH]
 
         def pick_last(g):
             pick_x(early[:, PACK - 1, g * CH : (g + 1) * CH], PACK - 1, g * CH, CH)
 
-        def pick_late(i):
-            pick_x(early[:, i, 0:CH], i, 3 * CH, CH)
-
         def round_x(g):
-            interleave(nc.scalar.copy, x_bf[g][:], picked(g))
+            interleave(nc.scalar.copy if g < 3 else nc.vector.tensor_copy, x_bf[g][:], picked(g))
 
         def quant_x(g):
             quantize(x_q[g][:], x_s[g][:], x_bf[g][:].rearrange("p c t -> p (c t)"))
@@ -224,33 +221,30 @@ def tile_list_htabg_glu_biasP_kernel(
             for s in range(WIDTHS[c] // SUB):
                 memory(c, s)
         for i in range(PACK - 1):
-            pick_x(early[:, i, :], i, 0, 3 * CH)
-        nc.vector.tensor_copy(ds[:].rearrange("p (t m) -> p t m", t=PACK), ds_raw[:].rearrange("p (m t) -> p t m", t=PACK))
+            pick_x(early[:, i, :], i, 0, J)
         pick_last(0)
         round_x(0)
         pick_last(1)
         round_x(1)
-        nc.vector.tensor_copy(
-            wd_q[:].rearrange("p (t m i) -> p m t i", t=PACK, i=4), wd_raw[:].rearrange("p (m i t) -> p m t i", t=PACK, i=4)
-        )
         pick_last(2)
         round_x(2)
         quant_x(0)
         gate(0)
-        pick_late(0)
-        pick_late(1)
+        pick_last(3)
         quant_x(1)
         gate(1)
-        pick_late(2)
-        pick_late(3)
         round_x(3)
+        nc.vector.tensor_copy(
+            wd_q[:].rearrange("p (t m i) -> p m t i", t=PACK, i=4), wd_raw[:].rearrange("p (m i t) -> p m t i", t=PACK, i=4)
+        )
+        nc.vector.tensor_copy(ds[:].rearrange("p (t m) -> p t m", t=PACK), ds_raw[:].rearrange("p (m t) -> p t m", t=PACK))
         quant_x(2)
-        join(0)
         gate(2)
-        down(0)
-        join(1)
+        join(0)
         quant_x(3)
+        down(0)
         gate(3)
+        join(1)
         down(1)
         join(2)
         round_y(0)
@@ -262,10 +256,12 @@ def tile_list_htabg_glu_biasP_kernel(
         round_y(1)
         down(4)
         emit(1)
-        for c in range(2, NCH):
-            round_y(c)
-        for c in range(2, NCH):
-            emit(c)
+        round_y(2)
+        round_y(3)
+        emit(2)
+        emit(3)
+        round_y(4)
+        emit(4)
         for q in range(4):
             queue = nc.scalar if q % 2 else nc.sync
             queue.dma_start(out_2[0, 4 * q : 4 * q + 4, :].bitcast(I32), out_s[32 * q : 32 * q + 4, :].bitcast(I32))

@@ -25,6 +25,8 @@ NCH = len(WIDTHS)
 HALF = J // 2
 CH = 256
 NG = J // CH
+CODE_STORES = {2: 0, 4: 768}
+LATE = (8, 9, 12, 9)
 
 
 def tile_list_htabg_glu_biasP_kernel(
@@ -48,7 +50,6 @@ def tile_list_htabg_glu_biasP_kernel(
         wgt = keep.tile([P, J], F32, align_bytes=64)
         wa_raw = keep.tile([P, PACK, R], F32, align_bytes=64)
         wa_bf = keep.tile([P, R * PACK], BF16, align_bytes=64)
-        wa_nat = keep.tile([P, R, PACK], BF16, align_bytes=64)
         wa_q = keep.tile([P, R], U32, align_bytes=64)
         wa_s = keep.tile([P, R], U8, align_bytes=64)
         wb_raw = keep.tile([P, 2, 2 * R], U8, align_bytes=64)
@@ -77,15 +78,17 @@ def tile_list_htabg_glu_biasP_kernel(
         for q in range(4):
             nc.sync.dma_start(tab_s[32 * q : 32 * q + 8, :].bitcast(I32), tab_scales[:, 4 * q : 4 * q + 4, :].bitcast(I32))
         nc.sync.dma_start(tab_w[:], tab_words[0].rearrange("p t b -> p (t b)").bitcast(I32))
-        nc.sync.dma_start(wa_raw[:], wa.rearrange("(p i) r -> p i r", i=PACK))
         for q in range(4):
             nc.sync.dma_start(
                 ws_raw[32 * q : 32 * q + 4, :, :].bitcast(I32),
                 wb_scales[:, 4 * q : 4 * q + 4, :].rearrange("a r c -> r a c").bitcast(I32),
             )
-        nc.sync.dma_start(idx2[:], offs2)
-        nc.sync.dma_start(wgt[:], wgt2)
+        nc.sync.dma_start(wa_raw[:], wa.rearrange("(p i) r -> p i r", i=PACK))
         nc.sync.dma_start(planes[0][:], x_rows[0])
+        nc.vector.tensor_copy(got_s[:], tab_s[:].indirect(idx[:]))
+        nc.sync.dma_start(got_s1[0:100, :].bitcast(I32), got_s[4:104, :].bitcast(I32))
+        nc.sync.dma_start(wgt[:], wgt2)
+        nc.sync.dma_start(idx2[:], offs2)
         nc.sync.dma_start(planes[1][:], x_rows[1])
         nc.sync.dma_start(planes[2][:], x_rows[2])
         nc.sync.dma_start(planes[3][:], x_rows[3])
@@ -100,18 +103,21 @@ def tile_list_htabg_glu_biasP_kernel(
             wb_q[:].bitcast(U16).rearrange("p a (t m) -> p a t m", t=PACK),
             wb_raw[:].bitcast(U16).rearrange("p a (m t) -> p a t m", t=PACK),
         )
-        nc.vector.tensor_copy(got_s[:], tab_s[:].indirect(idx[:]))
-        nc.scalar.dma_start(got_s1[0:100, :].bitcast(I32), got_s[4:104, :].bitcast(I32))
 
-        early = keep.tile([P, PACK, J], F32, align_bytes=64)
+        early = keep.tile([P, 22, CH], F32, align_bytes=64)
         x_q = [ring.tile([P, CH], U32, name="x_q", align_bytes=64) for g in range(NG)]
         x_s = [ring.tile([P, CH], U8, name="x_s", align_bytes=64) for g in range(NG)]
         x_bf = [ring.tile([P, CH, PACK], BF16, name="x_bf", align_bytes=64) for g in range(NG)]
         t_q = [keep.tile([P, 2, 2 * HALF], U8, name="t_q%d" % u, align_bytes=64) for u in range(2)]
         got_w = keep.tile([P, J], U32, align_bytes=64)
         h_bf = [ring.tile([P, w, PACK], BF16, name="h_bf", align_bytes=64) for w in WIDTHS]
+        h_q = [ring.tile([P, w], U32, name="h_q", align_bytes=64) for w in WIDTHS]
+        h_s = [ring.tile([P, w], U8, name="h_s", align_bytes=64) for w in WIDTHS]
+        y_q = keep.tile([P, J], I32, align_bytes=64)
         act = [ring.tile([P, w, PACK], F32, name="act", align_bytes=64) for w in WIDTHS]
-        yb_sb = [ring.tile([P, w, PACK], F32, name="yb_sb", align_bytes=64) for w in WIDTHS]
+        wa_flat = wa_raw[:].rearrange("p i r -> p (i r)")
+        yb_sb = [wa_flat[:, c * CH * PACK : (c + 1) * CH * PACK].rearrange("p (n t) -> p n t", t=PACK) for c in range(2)]
+        yb_sb = yb_sb + [ring.tile([P, w, PACK], F32, name="yb_sb", align_bytes=64)[:] for w in WIDTHS[2:]]
         y_sb = [ring.tile([P, PACK, w], F32, name="y_sb", align_bytes=64) for w in WIDTHS]
         y_bf = [ring.tile([P, w, PACK], BF16, name="y_bf", align_bytes=64) for w in WIDTHS]
 
@@ -130,14 +136,25 @@ def tile_list_htabg_glu_biasP_kernel(
         def pick_x(dst, i, j0, n):
             nc.vector.tensor_tensor(dst, planes[i][:].indirect(entries(idx2, j0, n)), wgt[:, j0 : j0 + n], MULT)
 
-        def picked(g):
-            return early[:, :, g * CH : (g + 1) * CH]
-
-        def pick_last(g):
-            pick_x(early[:, PACK - 1, g * CH : (g + 1) * CH], PACK - 1, g * CH, CH)
+        def pick_late(i, g):
+            pick_x(early[:, LATE[g] + 4 * (i - 2), :], i, g * CH, CH)
 
         def round_x(g):
-            interleave(nc.scalar.copy if g < 3 else nc.vector.tensor_copy, x_bf[g][:], picked(g))
+            step = LATE[g] - g
+            src = early[:, g : g + 2 * step, :].rearrange("p (a x) c -> p a x c", a=2)[:, :, 0:5:4, :]
+            nc.scalar.copy(
+                x_bf[g][:].rearrange("p (c i) (a e) -> p c a e i", i=4, a=2),
+                src.rearrange("p a e (c i) -> p c a e i", i=4),
+            )
+
+        def deal_wd():
+            nc.vector.tensor_copy(
+                wd_q[:].rearrange("p (t m i) -> p m t i", t=PACK, i=4),
+                wd_raw[:].rearrange("p (m i t) -> p m t i", t=PACK, i=4),
+            )
+            nc.vector.tensor_copy(
+                ds[:].rearrange("p (t m) -> p t m", t=PACK), ds_raw[:].rearrange("p (m t) -> p t m", t=PACK)
+            )
 
         def quant_x(g):
             quantize(x_q[g][:], x_s[g][:], x_bf[g][:].rearrange("p c t -> p (c t)"))
@@ -176,21 +193,21 @@ def tile_list_htabg_glu_biasP_kernel(
                 nc.scalar.activation(dst, ya[:].rearrange("p t n -> p n t"), ACT.Silu)
 
         def join(c):
-            nc.vector.tensor_tensor(h_bf[c][:], act[c][:], yb_sb[c][:], MULT)
+            nc.vector.tensor_tensor(h_bf[c][:], act[c][:], yb_sb[c], MULT)
+
+        def quant_h(c):
+            quantize(h_q[c][:], h_s[c][:], h_bf[c][:].rearrange("p c t -> p (c t)"))
 
         def down(c):
             w = WIDTHS[c]
             per_bank = 512 // w
-            h_q = ring.tile([P, w], U32, name="h_q", align_bytes=64)
-            h_s = ring.tile([P, w], U8, name="h_s", align_bytes=64)
-            quantize(h_q[:], h_s[:], h_bf[c][:].rearrange("p c t -> p (c t)"))
             for t0 in range(0, PACK, per_bank):
                 y = psum.tile([P, per_bank, w], F32, name="bank")
                 for e in range(per_bank):
                     m = slice((t0 + e) * P, (t0 + e + 1) * P)
                     nc.tensor.matmul_mx(
                         out=y[:, e, :], lhsT=wd_q[:, m].bitcast(FP8X4), lhsT_scale=ds[:, m],
-                        rhs=h_q[:].bitcast(FP8X4), rhs_scale=h_s[:], start=True, stop=True,
+                        rhs=h_q[c][:].bitcast(FP8X4), rhs_scale=h_s[c][:], start=True, stop=True,
                     )
                 for e in range(per_bank):
                     t = t0 + e
@@ -201,9 +218,10 @@ def tile_list_htabg_glu_biasP_kernel(
             interleave(nc.vector.tensor_copy, y_bf[c][:], y_sb[c][:])
 
         def emit(c):
-            y_q = ring.tile([P, WIDTHS[c]], I32, name="y_q", align_bytes=64)
-            quantize(y_q[:], out_s[:, cols(c)], y_bf[c][:].rearrange("p c t -> p (c t)"))
-            nc.sync.dma_start(out_1[0].rearrange("p j b -> p (j b)").bitcast(I32)[:, cols(c)], y_q[:])
+            quantize(y_q[:, cols(c)], out_s[:, cols(c)], y_bf[c][:].rearrange("p c t -> p (c t)"))
+            if c in CODE_STORES:
+                span = slice(CODE_STORES[c], STARTS[c] + WIDTHS[c])
+                nc.sync.dma_start(out_1[0].rearrange("p j b -> p (j b)").bitcast(I32)[:, span], y_q[:, span])
 
         nc.vector.tensor_copy(got_w[:], tab_w[:].bitcast(U32).indirect(idx[:]))
         for u in range(2):
@@ -211,54 +229,59 @@ def tile_list_htabg_glu_biasP_kernel(
         nc.vector.tensor_copy(
             ws[:].rearrange("p a (t m) -> p a t m", t=PACK), ws_raw[:].rearrange("p a (m t) -> p a t m", t=PACK)
         )
-        interleave(nc.scalar.copy, wa_nat[:], wa_raw[:])
         nc.scalar.copy(
-            wa_bf[:].bitcast(F32).rearrange("p (t m e) -> p t m e", t=PACK, e=2),
-            wa_nat[:].rearrange("p r i -> p (r i)").bitcast(F32).rearrange("p (m t e) -> p t m e", t=PACK, e=2),
+            wa_bf[:].rearrange("p (t m i) -> p m i t", t=PACK, i=PACK),
+            wa_raw[:].rearrange("p i (m t) -> p m i t", t=PACK),
         )
         quantize(wa_q[:], wa_s[:], wa_bf[:])
         for c in range(NCH):
             for s in range(WIDTHS[c] // SUB):
                 memory(c, s)
-        for i in range(PACK - 1):
-            pick_x(early[:, i, :], i, 0, J)
-        pick_last(0)
+        for i in range(2):
+            pick_x(early[:, 4 * i : 4 * i + 4, :].rearrange("p s c -> p (s c)"), i, 0, J)
+        pick_late(2, 0)
+        pick_late(2, 1)
+        pick_late(3, 0)
         round_x(0)
-        pick_last(1)
+        pick_late(3, 1)
         round_x(1)
-        pick_last(2)
-        round_x(2)
         quant_x(0)
         gate(0)
-        pick_last(3)
+        pick_late(3, 2)
+        pick_late(2, 2)
         quant_x(1)
+        round_x(2)
         gate(1)
-        round_x(3)
-        nc.vector.tensor_copy(
-            wd_q[:].rearrange("p (t m i) -> p m t i", t=PACK, i=4), wd_raw[:].rearrange("p (m i t) -> p m t i", t=PACK, i=4)
-        )
-        nc.vector.tensor_copy(ds[:].rearrange("p (t m) -> p t m", t=PACK), ds_raw[:].rearrange("p (m t) -> p t m", t=PACK))
-        quant_x(2)
-        gate(2)
+        pick_late(2, 3)
+        pick_late(3, 3)
+        deal_wd()
         join(0)
+        quant_x(2)
+        quant_h(0)
+        round_x(3)
+        join(1)
+        gate(2)
         quant_x(3)
+        quant_h(1)
         down(0)
         gate(3)
-        join(1)
-        down(1)
         join(2)
-        round_y(0)
-        down(2)
+        quant_h(2)
+        down(1)
         join(3)
-        emit(0)
         join(4)
+        quant_h(3)
+        quant_h(4)
+        down(2)
+        round_y(0)
+        emit(0)
         down(3)
         round_y(1)
-        down(4)
         emit(1)
+        down(4)
         round_y(2)
-        round_y(3)
         emit(2)
+        round_y(3)
         emit(3)
         round_y(4)
         emit(4)

@@ -1,6 +1,7 @@
 from contextlib import ExitStack
 
 import concourse.mybir as mybir
+from concourse.masks import make_identity
 
 K, L, R, N, T, J = 512, 1024, 512, 512, 2048, 1024
 FLOPS = 2 * J * (K * R + L * R + R * N)
@@ -26,7 +27,7 @@ HALF = J // 2
 CH = 256
 NG = J // CH
 CODE_STORES = {2: 0, 4: 768}
-LATE = (8, 9, 12, 9)
+LATE = (8, 9, 10, 9)
 
 
 def tile_list_htabg_glu_biasP_kernel(
@@ -38,7 +39,8 @@ def tile_list_htabg_glu_biasP_kernel(
         lists = ctx.enter_context(tc.tile_pool(name="lists", bufs=1))
         keep = ctx.enter_context(tc.tile_pool(name="keep", bufs=1))
         ring = ctx.enter_context(tc.tile_pool(name="ring", bufs=NCH))
-        psum = ctx.enter_context(tc.psum_pool(name="psum", bufs=8))
+        psum = ctx.enter_context(tc.psum_pool(name="psum", bufs=5))
+        psum_yb = ctx.enter_context(tc.psum_pool(name="psum_yb", bufs=3))
 
         idx = lists.tile([P, J // 16], U16)
         idx2 = lists.tile([P, J // 16], U16)
@@ -48,15 +50,16 @@ def tile_list_htabg_glu_biasP_kernel(
         got_s1 = keep.tile([P, J], U8, align_bytes=64)
         planes = [keep.tile([P, T], F32, name="x_plane%d" % i, align_bytes=64) for i in range(PACK)]
         wgt = keep.tile([P, J], F32, align_bytes=64)
-        wa_raw = keep.tile([P, PACK, R], F32, align_bytes=64)
+        wgt_rows = keep.tile([P, P], F32, align_bytes=64)
+        wgt_wide = keep.tile([P, 8, P], F32, align_bytes=64)
+        ident = keep.tile([P, P], F32, align_bytes=64)
+        wa_raw = [keep.tile([P, PACK, R // 2], F32, name="wa_raw%d" % u, align_bytes=64) for u in range(2)]
         wa_bf = keep.tile([P, R * PACK], BF16, align_bytes=64)
         wa_q = keep.tile([P, R], U32, align_bytes=64)
         wa_s = keep.tile([P, R], U8, align_bytes=64)
-        wb_raw = keep.tile([P, 2, 2 * R], U8, align_bytes=64)
         wb_q = keep.tile([P, 2, 2 * R], U8, align_bytes=64)
         wd_raw = keep.tile([P, N], I32, align_bytes=64)
         wd_q = keep.tile([P, N], I32, align_bytes=64)
-        ws_raw = keep.tile([P, 2, R], U8, align_bytes=64)
         ws = keep.tile([P, 2, R], U8, align_bytes=64)
         ds_raw = keep.tile([P, N], U8, align_bytes=64)
         ds = keep.tile([P, N], U8, align_bytes=64)
@@ -68,27 +71,33 @@ def tile_list_htabg_glu_biasP_kernel(
         nc.gpsimd.memset(tab_s[:].bitcast(I32), 0)
         nc.vector.memset(zero[:], 0.0)
         nc.scalar.activation(warm[:], zero[:], ACT.Silu)
-        nc.gpsimd.memset(ws_raw[:].rearrange("p a r -> p (a r)").bitcast(I32), 0)
+        nc.gpsimd.memset(wgt_rows[64:128, :], 0.0)
+        make_identity(nc, ident[:])
+        nc.gpsimd.memset(ws[:].rearrange("p a r -> p (a r)").bitcast(I32), 0)
         nc.gpsimd.memset(ds_raw[:].bitcast(I32), 0)
         nc.gpsimd.memset(got_s1[:].bitcast(I32), 0)
 
         x_rows = xT.rearrange("(p i) t -> i p t", i=PACK)
         nc.sync.dma_start(idx[:], offs)
-        nc.sync.dma_start(wb_raw[:].bitcast(I32), wb_words.rearrange("a p c -> p a c").bitcast(I32))
-        for q in range(4):
-            nc.sync.dma_start(tab_s[32 * q : 32 * q + 8, :].bitcast(I32), tab_scales[:, 4 * q : 4 * q + 4, :].bitcast(I32))
+        nc.sync.dma_start(wb_q[:].bitcast(I32), wb_words.rearrange("a p c -> p a c").bitcast(I32))
+        for r in range(4):
+            nc.sync.dma_start(
+                tab_s[r:P:16, :].bitcast(I32), tab_scales[:, r:16:4, :].rearrange("a q t -> q a t").bitcast(I32)
+            )
+        nc.sync.dma_start(wgt_rows[0:64, :], wgt2[0:P:16, :].rearrange("g (e j) -> g e j", e=8))
         nc.sync.dma_start(tab_w[:], tab_words[0].rearrange("p t b -> p (t b)").bitcast(I32))
+        nc.sync.dma_start(idx2[:], offs2)
+        wa_rows = wa.rearrange("(p i) r -> p i r", i=PACK)
+        nc.sync.dma_start(wa_raw[0][:], wa_rows[:, :, 0 : R // 2])
+        nc.sync.dma_start(planes[0][:], x_rows[0])
         for q in range(4):
             nc.sync.dma_start(
-                ws_raw[32 * q : 32 * q + 4, :, :].bitcast(I32),
+                ws[32 * q : 32 * q + 4, :, :].bitcast(I32),
                 wb_scales[:, 4 * q : 4 * q + 4, :].rearrange("a r c -> r a c").bitcast(I32),
             )
-        nc.sync.dma_start(wa_raw[:], wa.rearrange("(p i) r -> p i r", i=PACK))
-        nc.sync.dma_start(planes[0][:], x_rows[0])
+        nc.sync.dma_start(wa_raw[1][:], wa_rows[:, :, R // 2 : R])
         nc.vector.tensor_copy(got_s[:], tab_s[:].indirect(idx[:]))
-        nc.sync.dma_start(got_s1[0:100, :].bitcast(I32), got_s[4:104, :].bitcast(I32))
-        nc.sync.dma_start(wgt[:], wgt2)
-        nc.sync.dma_start(idx2[:], offs2)
+        nc.sync.dma_start(got_s1[0:100, :].bitcast(I32), got_s[16:116, :].bitcast(I32))
         nc.sync.dma_start(planes[1][:], x_rows[1])
         nc.sync.dma_start(planes[2][:], x_rows[2])
         nc.sync.dma_start(planes[3][:], x_rows[3])
@@ -99,10 +108,18 @@ def tile_list_htabg_glu_biasP_kernel(
         nc.sync.dma_start(wd_raw[:], wd_words[0].rearrange("p n b -> p (n b)").bitcast(I32))
         nc.sync.dma_start(bias[:], b.rearrange("(p t) -> p t", t=PACK))
 
-        nc.vector.tensor_copy(
-            wb_q[:].bitcast(U16).rearrange("p a (t m) -> p a t m", t=PACK),
-            wb_raw[:].bitcast(U16).rearrange("p a (m t) -> p a t m", t=PACK),
+        turned = psum.tile([P, P], F32, name="bank")
+        nc.tensor.transpose(turned[:], wgt_rows[:], ident[:])
+        nc.scalar.copy(
+            wgt_wide[:].rearrange("p e (g d) -> p e g d", d=16),
+            turned[:, 0:64].rearrange("p (g e) -> p e g", e=8).unsqueeze(3).to_broadcast([P, 8, 8, 16]),
         )
+        for u in range(2):
+            back = psum.tile([P, PACK, P], F32, name="bank")
+            for e in range(PACK):
+                nc.tensor.transpose(back[:, e, :], wgt_wide[:, PACK * u + e, :], ident[:])
+            nc.scalar.copy(wgt[:, u * HALF : (u + 1) * HALF], back[:].rearrange("p e j -> p (e j)"))
+
 
         early = keep.tile([P, 22, CH], F32, align_bytes=64)
         x_q = [ring.tile([P, CH], U32, name="x_q", align_bytes=64) for g in range(NG)]
@@ -115,9 +132,9 @@ def tile_list_htabg_glu_biasP_kernel(
         h_s = [ring.tile([P, w], U8, name="h_s", align_bytes=64) for w in WIDTHS]
         y_q = keep.tile([P, J], I32, align_bytes=64)
         act = [ring.tile([P, w, PACK], F32, name="act", align_bytes=64) for w in WIDTHS]
-        wa_flat = wa_raw[:].rearrange("p i r -> p (i r)")
-        yb_sb = [wa_flat[:, c * CH * PACK : (c + 1) * CH * PACK].rearrange("p (n t) -> p n t", t=PACK) for c in range(2)]
-        yb_sb = yb_sb + [ring.tile([P, w, PACK], F32, name="yb_sb", align_bytes=64)[:] for w in WIDTHS[2:]]
+        yb_last = keep.tile([P, 6, R], F32, align_bytes=64)
+        wa_place = wa_raw[1][:].rearrange("p (s i) r -> p s (i r)", s=2)
+        yb_t = [wa_place[:, s, :] for s in range(2)] + [yb_last[:, s, :] for s in range(6)]
         y_sb = [ring.tile([P, PACK, w], F32, name="y_sb", align_bytes=64) for w in WIDTHS]
         y_bf = [ring.tile([P, w, PACK], BF16, name="y_bf", align_bytes=64) for w in WIDTHS]
 
@@ -165,19 +182,17 @@ def tile_list_htabg_glu_biasP_kernel(
                 got_w[:, u * HALF : (u + 1) * HALF].bitcast(U16).rearrange("p (j d) -> p d j", d=2),
             )
 
-        def memory(c, s):
-            yb = psum.tile([P, PACK, SUB], F32, name="bank")
-            j0 = STARTS[c] + s * SUB
+        def memory(s):
+            yb = psum.tile([P, R], F32, name="bank") if s < 5 else psum_yb.tile([P, R], F32, name="yb_bank")
+            j0 = s * SUB
             jh = j0 % HALF
-            for t in range(PACK):
-                for a in range(2):
-                    nc.tensor.matmul_mx(
-                        out=yb[:, t, :], lhsT=wb_q[:, a, 2 * t * P : 2 * (t + 1) * P].bitcast(FP4X4),
-                        lhsT_scale=ws[:, a, t * P : (t + 1) * P],
-                        rhs=t_q[j0 // HALF][:, a, 2 * jh : 2 * (jh + SUB)].bitcast(FP4X4),
-                        rhs_scale=(got_s, got_s1)[a][:, j0 : j0 + SUB], start=(a == 0), stop=(a == 1),
-                    )
-            nc.scalar.copy(yb_sb[c][:, s * SUB : (s + 1) * SUB, :], yb[:].rearrange("p t n -> p n t"))
+            for a in range(2):
+                nc.tensor.matmul_mx(
+                    out=yb[:], lhsT=t_q[j0 // HALF][:, a, 2 * jh : 2 * (jh + SUB)].bitcast(FP4X4),
+                    lhsT_scale=(got_s, got_s1)[a][:, j0 : j0 + SUB],
+                    rhs=wb_q[:, a, :].bitcast(FP4X4), rhs_scale=ws[:, a, :], start=(a == 0), stop=(a == 1),
+                )
+            nc.scalar.copy(yb_t[s].rearrange("p (t m) -> p t m", t=PACK), yb[:].rearrange("p (m t) -> p t m", t=PACK))
 
         def gate(g):
             for s in range(CH // SUB):
@@ -193,7 +208,12 @@ def tile_list_htabg_glu_biasP_kernel(
                 nc.scalar.activation(dst, ya[:].rearrange("p t n -> p n t"), ACT.Silu)
 
         def join(c):
-            nc.vector.tensor_tensor(h_bf[c][:], act[c][:], yb_sb[c], MULT)
+            for s in range(WIDTHS[c] // SUB):
+                sub = slice(s * SUB, (s + 1) * SUB)
+                yb = psum_yb.tile([P, PACK, SUB], F32, name="yb_bank")
+                for t in range(PACK):
+                    nc.tensor.transpose(yb[:, t, :], yb_t[STARTS[c] // SUB + s][:, t * P : (t + 1) * P], ident[:])
+                nc.vector.tensor_tensor(h_bf[c][:, sub, :], act[c][:, sub, :], yb[:].rearrange("p t n -> p n t"), MULT)
 
         def quant_h(c):
             quantize(h_q[c][:], h_s[c][:], h_bf[c][:].rearrange("p c t -> p (c t)"))
@@ -226,21 +246,19 @@ def tile_list_htabg_glu_biasP_kernel(
         nc.vector.tensor_copy(got_w[:], tab_w[:].bitcast(U32).indirect(idx[:]))
         for u in range(2):
             part_tab(u)
-        nc.vector.tensor_copy(
-            ws[:].rearrange("p a (t m) -> p a t m", t=PACK), ws_raw[:].rearrange("p a (m t) -> p a t m", t=PACK)
-        )
-        nc.scalar.copy(
-            wa_bf[:].rearrange("p (t m i) -> p m i t", t=PACK, i=PACK),
-            wa_raw[:].rearrange("p i (m t) -> p m i t", t=PACK),
-        )
+        for u in range(2):
+            nc.scalar.copy(
+                wa_bf[:].rearrange("p (t u m i) -> p u m i t", t=PACK, u=2, i=PACK)[:, u],
+                wa_raw[u][:].rearrange("p i (m t) -> p m i t", t=PACK),
+            )
         quantize(wa_q[:], wa_s[:], wa_bf[:])
-        for c in range(NCH):
-            for s in range(WIDTHS[c] // SUB):
-                memory(c, s)
+        for s in range(J // SUB):
+            memory(s)
         for i in range(2):
             pick_x(early[:, 4 * i : 4 * i + 4, :].rearrange("p s c -> p (s c)"), i, 0, J)
         pick_late(2, 0)
         pick_late(2, 1)
+        pick_late(2, 2)
         pick_late(3, 0)
         round_x(0)
         pick_late(3, 1)
@@ -248,7 +266,6 @@ def tile_list_htabg_glu_biasP_kernel(
         quant_x(0)
         gate(0)
         pick_late(3, 2)
-        pick_late(2, 2)
         quant_x(1)
         round_x(2)
         gate(1)

@@ -26,7 +26,6 @@ NCH = len(WIDTHS)
 HALF = J // 2
 CH = 256
 NG = J // CH
-CODE_STORES = {2: 0, 4: 768}
 LATE = (8, 9, 10, 9)
 
 
@@ -125,7 +124,7 @@ def tile_list_htabg_glu_biasP_kernel(
         x_q = [ring.tile([P, CH], U32, name="x_q", align_bytes=64) for g in range(NG)]
         x_s = [ring.tile([P, CH], U8, name="x_s", align_bytes=64) for g in range(NG)]
         x_bf = [ring.tile([P, CH, PACK], BF16, name="x_bf", align_bytes=64) for g in range(NG)]
-        t_q = [keep.tile([P, 2, 2 * HALF], U8, name="t_q%d" % u, align_bytes=64) for u in range(2)]
+        t_q = keep.tile([P, 2, 2 * J], U8, align_bytes=64)
         got_w = keep.tile([P, J], U32, align_bytes=64)
         h_bf = [ring.tile([P, w, PACK], BF16, name="h_bf", align_bytes=64) for w in WIDTHS]
         h_q = [ring.tile([P, w], U32, name="h_q", align_bytes=64) for w in WIDTHS]
@@ -135,8 +134,8 @@ def tile_list_htabg_glu_biasP_kernel(
         yb_last = keep.tile([P, 6, R], F32, align_bytes=64)
         wa_place = wa_raw[1][:].rearrange("p (s i) r -> p s (i r)", s=2)
         yb_t = [wa_place[:, s, :] for s in range(2)] + [yb_last[:, s, :] for s in range(6)]
-        y_sb = [ring.tile([P, PACK, w], F32, name="y_sb", align_bytes=64) for w in WIDTHS]
-        y_bf = [ring.tile([P, w, PACK], BF16, name="y_bf", align_bytes=64) for w in WIDTHS]
+        y_sb = keep.tile([P, PACK, J], F32, align_bytes=64)
+        y_bf = keep.tile([P, J, PACK], BF16, align_bytes=64)
 
         def cols(c):
             return slice(STARTS[c], STARTS[c] + WIDTHS[c])
@@ -153,8 +152,9 @@ def tile_list_htabg_glu_biasP_kernel(
         def pick_x(dst, i, j0, n):
             nc.vector.tensor_tensor(dst, planes[i][:].indirect(entries(idx2, j0, n)), wgt[:, j0 : j0 + n], MULT)
 
-        def pick_late(i, g):
-            pick_x(early[:, LATE[g] + 4 * (i - 2), :], i, g * CH, CH)
+        def pick_late(i, g, n):
+            first = LATE[g] + 4 * (i - 2)
+            pick_x(early[:, first : first + n, :].rearrange("p s c -> p (s c)"), i, g * CH, n * CH)
 
         def round_x(g):
             step = LATE[g] - g
@@ -176,26 +176,19 @@ def tile_list_htabg_glu_biasP_kernel(
         def quant_x(g):
             quantize(x_q[g][:], x_s[g][:], x_bf[g][:].rearrange("p c t -> p (c t)"))
 
-        def part_tab(u):
-            nc.vector.tensor_copy(
-                t_q[u][:].bitcast(U16),
-                got_w[:, u * HALF : (u + 1) * HALF].bitcast(U16).rearrange("p (j d) -> p d j", d=2),
-            )
-
         def memory(s):
             yb = psum.tile([P, R], F32, name="bank") if s < 5 else psum_yb.tile([P, R], F32, name="yb_bank")
             j0 = s * SUB
-            jh = j0 % HALF
             for a in range(2):
                 nc.tensor.matmul_mx(
-                    out=yb[:], lhsT=t_q[j0 // HALF][:, a, 2 * jh : 2 * (jh + SUB)].bitcast(FP4X4),
+                    out=yb[:], lhsT=t_q[:, a, 2 * j0 : 2 * (j0 + SUB)].bitcast(FP4X4),
                     lhsT_scale=(got_s, got_s1)[a][:, j0 : j0 + SUB],
                     rhs=wb_q[:, a, :].bitcast(FP4X4), rhs_scale=ws[:, a, :], start=(a == 0), stop=(a == 1),
                 )
             nc.scalar.copy(yb_t[s].rearrange("p (t m) -> p t m", t=PACK), yb[:].rearrange("p (m t) -> p t m", t=PACK))
 
-        def gate(g):
-            for s in range(CH // SUB):
+        def gate(g, subs=(0, 1)):
+            for s in subs:
                 sub = slice(s * SUB, (s + 1) * SUB)
                 ya = psum.tile([P, PACK, SUB], F32, name="bank")
                 for t in range(PACK):
@@ -231,21 +224,29 @@ def tile_list_htabg_glu_biasP_kernel(
                     )
                 for e in range(per_bank):
                     t = t0 + e
-                    nc.scalar.activation(y_sb[c][:, t, :], y[:, e, :], ACT.Identity, bias=bias[:, t : t + 1])
-            nc.sync.dma_start(out_0.rearrange("(p t) j -> p t j", t=PACK)[:, :, cols(c)], y_sb[c][:])
+                    nc.scalar.activation(y_sb[:, t, cols(c)], y[:, e, :], ACT.Identity, bias=bias[:, t : t + 1])
+                if per_bank < PACK:
+                    rows = slice(t0, t0 + per_bank)
+                    nc.sync.dma_start(out_0.rearrange("(p t) j -> p t j", t=PACK)[:, rows, cols(c)], y_sb[:, rows, cols(c)])
 
-        def round_y(c):
-            interleave(nc.vector.tensor_copy, y_bf[c][:], y_sb[c][:])
+        def store_y(j0, j1):
+            nc.sync.dma_start(out_0.rearrange("(p t) j -> p t j", t=PACK)[:, :, j0:j1], y_sb[:, :, j0:j1])
 
-        def emit(c):
-            quantize(y_q[:, cols(c)], out_s[:, cols(c)], y_bf[c][:].rearrange("p c t -> p (c t)"))
-            if c in CODE_STORES:
-                span = slice(CODE_STORES[c], STARTS[c] + WIDTHS[c])
-                nc.sync.dma_start(out_1[0].rearrange("p j b -> p (j b)").bitcast(I32)[:, span], y_q[:, span])
+        def round_y(copy, j0, j1):
+            interleave(copy, y_bf[:, j0:j1, :], y_sb[:, :, j0:j1])
+
+        def quant_y(j0, j1):
+            quantize(y_q[:, j0:j1], out_s[:, j0:j1], y_bf[:, j0:j1, :].rearrange("p c t -> p (c t)"))
+
+        def store_codes(j0, j1):
+            nc.sync.dma_start(out_1[0].rearrange("p j b -> p (j b)").bitcast(I32)[:, j0:j1], y_q[:, j0:j1])
 
         nc.vector.tensor_copy(got_w[:], tab_w[:].bitcast(U32).indirect(idx[:]))
         for u in range(2):
-            part_tab(u)
+            half = slice(u * HALF, (u + 1) * HALF)
+            nc.vector.tensor_copy(
+                t_q[:].bitcast(U16)[:, :, half], got_w[:, half].bitcast(U16).rearrange("p (j d) -> p d j", d=2)
+            )
         for u in range(2):
             nc.scalar.copy(
                 wa_bf[:].rearrange("p (t u m i) -> p u m i t", t=PACK, u=2, i=PACK)[:, u],
@@ -256,21 +257,19 @@ def tile_list_htabg_glu_biasP_kernel(
             memory(s)
         for i in range(2):
             pick_x(early[:, 4 * i : 4 * i + 4, :].rearrange("p s c -> p (s c)"), i, 0, J)
-        pick_late(2, 0)
-        pick_late(2, 1)
-        pick_late(2, 2)
-        pick_late(3, 0)
+        pick_late(2, 0, 3)
+        pick_late(3, 0, 1)
         round_x(0)
-        pick_late(3, 1)
+        pick_late(3, 1, 1)
         round_x(1)
         quant_x(0)
         gate(0)
-        pick_late(3, 2)
+        pick_late(3, 2, 1)
         quant_x(1)
         round_x(2)
         gate(1)
-        pick_late(2, 3)
-        pick_late(3, 3)
+        pick_late(2, 3, 1)
+        pick_late(3, 3, 1)
         deal_wd()
         join(0)
         quant_x(2)
@@ -290,18 +289,23 @@ def tile_list_htabg_glu_biasP_kernel(
         quant_h(3)
         quant_h(4)
         down(2)
-        round_y(0)
-        emit(0)
+        round_y(nc.vector.tensor_copy, 0, 256)
+        quant_y(0, 256)
+        store_codes(0, 256)
+        round_y(nc.vector.tensor_copy, 256, 512)
         down(3)
-        round_y(1)
-        emit(1)
+        store_y(768, 896)
+        quant_y(256, 512)
         down(4)
-        round_y(2)
-        emit(2)
-        round_y(3)
-        emit(3)
-        round_y(4)
-        emit(4)
+        store_y(896, 1024)
+        round_y(nc.vector.tensor_copy, 512, 768)
+        quant_y(512, 768)
+        store_codes(256, 768)
+        round_y(nc.vector.tensor_copy, 768, 896)
+        quant_y(768, 896)
+        round_y(nc.scalar.copy, 896, 1024)
+        quant_y(896, 1024)
+        store_codes(768, 1024)
         for q in range(4):
             queue = nc.scalar if q % 2 else nc.sync
             queue.dma_start(out_2[0, 4 * q : 4 * q + 4, :].bitcast(I32), out_s[32 * q : 32 * q + 4, :].bitcast(I32))

@@ -16,6 +16,7 @@ FP8X4 = mybir.dt.float8_e4m3fn_x4
 FP4X4 = mybir.dt.float4_e2m1fn_x4
 ACT = mybir.ActivationFunctionType
 MULT = mybir.AluOpType.mult
+ADD = mybir.AluOpType.add
 
 P = 128
 PACK = 4
@@ -229,6 +230,19 @@ def tile_list_htabg_glu_biasP_kernel(
                     rows = slice(t0, t0 + per_bank)
                     nc.sync.dma_start(out_0.rearrange("(p t) j -> p t j", t=PACK)[:, rows, cols(c)], y_sb[:, rows, cols(c)])
 
+        def round_from_sums(c):
+            y = psum.tile([P, PACK, SUB], F32, name="bank")
+            for t in range(PACK):
+                m = slice(t * P, (t + 1) * P)
+                nc.tensor.matmul_mx(
+                    out=y[:, t, :], lhsT=wd_q[:, m].bitcast(FP8X4), lhsT_scale=ds[:, m],
+                    rhs=h_q[c][:].bitcast(FP8X4), rhs_scale=h_s[c][:], start=True, stop=True,
+                )
+            nc.vector.tensor_tensor(
+                y_bf[:, cols(c), :], y[:].rearrange("p t n -> p n t"),
+                bias[:].unsqueeze(1).to_broadcast([P, SUB, PACK]), ADD,
+            )
+
         def store_y(j0, j1):
             nc.sync.dma_start(out_0.rearrange("(p t) j -> p t j", t=PACK)[:, :, j0:j1], y_sb[:, :, j0:j1])
 
@@ -303,7 +317,7 @@ def tile_list_htabg_glu_biasP_kernel(
         store_codes(256, 768)
         round_y(nc.vector.tensor_copy, 768, 896)
         quant_y(768, 896)
-        round_y(nc.scalar.copy, 896, 1024)
+        round_from_sums(4)
         quant_y(896, 1024)
         store_codes(768, 1024)
         for q in range(4):

@@ -20,14 +20,18 @@ ADD = mybir.AluOpType.add
 
 P = 128
 PACK = 4
-SUB = 128
-WIDTHS = (256, 256, 256, 128, 128)
-STARTS = (0, 256, 512, 768, 896)
-NCH = len(WIDTHS)
+BANK = 512
+SUB = BANK // PACK
+HEADS = 8
 HALF = J // 2
-CH = 256
-NG = J // CH
+GROUP = 256
+GROUPS = J // GROUP
+WIDTHS = (256, 256, 256, 128, 128)
+STARTS = tuple(sum(WIDTHS[:c]) for c in range(len(WIDTHS)))
+CHUNKS = len(WIDTHS)
 LATE = (8, 9, 10, 9)
+PLACES = 2 * max(LATE)
+YB_BANKS = 3
 
 
 def tile_list_htabg_glu_biasP_kernel(
@@ -38,9 +42,9 @@ def tile_list_htabg_glu_biasP_kernel(
     with ExitStack() as ctx:
         lists = ctx.enter_context(tc.tile_pool(name="lists", bufs=1))
         keep = ctx.enter_context(tc.tile_pool(name="keep", bufs=1))
-        ring = ctx.enter_context(tc.tile_pool(name="ring", bufs=NCH))
-        psum = ctx.enter_context(tc.psum_pool(name="psum", bufs=5))
-        psum_yb = ctx.enter_context(tc.psum_pool(name="psum_yb", bufs=3))
+        ring = ctx.enter_context(tc.tile_pool(name="ring", bufs=CHUNKS))
+        psum = ctx.enter_context(tc.psum_pool(name="psum", bufs=8 - YB_BANKS))
+        psum_yb = ctx.enter_context(tc.psum_pool(name="psum_yb", bufs=YB_BANKS))
 
         idx = lists.tile([P, J // 16], U16)
         idx2 = lists.tile([P, J // 16], U16)
@@ -51,7 +55,7 @@ def tile_list_htabg_glu_biasP_kernel(
         planes = [keep.tile([P, T], F32, name="x_plane%d" % i, align_bytes=64) for i in range(PACK)]
         wgt = keep.tile([P, J], F32, align_bytes=64)
         wgt_rows = keep.tile([P, P], F32, align_bytes=64)
-        wgt_wide = keep.tile([P, 8, P], F32, align_bytes=64)
+        wgt_wide = keep.tile([P, J // P, P], F32, align_bytes=64)
         ident = keep.tile([P, P], F32, align_bytes=64)
         wa_raw = [keep.tile([P, PACK, R // 2], F32, name="wa_raw%d" % u, align_bytes=64) for u in range(2)]
         wa_bf = keep.tile([P, R * PACK], BF16, align_bytes=64)
@@ -60,9 +64,9 @@ def tile_list_htabg_glu_biasP_kernel(
         wb_q = keep.tile([P, 2, 2 * R], U8, align_bytes=64)
         wd_raw = keep.tile([P, N], I32, align_bytes=64)
         wd_q = keep.tile([P, N], I32, align_bytes=64)
-        ws = keep.tile([P, 2, R], U8, align_bytes=64)
-        ds_raw = keep.tile([P, N], U8, align_bytes=64)
-        ds = keep.tile([P, N], U8, align_bytes=64)
+        wb_s = keep.tile([P, 2, R], U8, align_bytes=64)
+        wd_s_raw = keep.tile([P, N], U8, align_bytes=64)
+        wd_s = keep.tile([P, N], U8, align_bytes=64)
         bias = keep.tile([P, PACK], F32, align_bytes=64)
         zero = keep.tile([P, 1], F32, align_bytes=64)
         warm = keep.tile([P, 1], F32, align_bytes=64)
@@ -71,10 +75,10 @@ def tile_list_htabg_glu_biasP_kernel(
         nc.gpsimd.memset(tab_s[:].bitcast(I32), 0)
         nc.vector.memset(zero[:], 0.0)
         nc.scalar.activation(warm[:], zero[:], ACT.Silu)
-        nc.gpsimd.memset(wgt_rows[64:128, :], 0.0)
+        nc.gpsimd.memset(wgt_rows[P // 2 : P, :], 0.0)
         make_identity(nc, ident[:])
-        nc.gpsimd.memset(ws[:].rearrange("p a r -> p (a r)").bitcast(I32), 0)
-        nc.gpsimd.memset(ds_raw[:].bitcast(I32), 0)
+        nc.gpsimd.memset(wb_s[:].rearrange("p a r -> p (a r)").bitcast(I32), 0)
+        nc.gpsimd.memset(wd_s_raw[:].bitcast(I32), 0)
         nc.gpsimd.memset(got_s1[:].bitcast(I32), 0)
 
         x_rows = xT.rearrange("(p i) t -> i p t", i=PACK)
@@ -84,7 +88,7 @@ def tile_list_htabg_glu_biasP_kernel(
             nc.sync.dma_start(
                 tab_s[r:P:16, :].bitcast(I32), tab_scales[:, r:16:4, :].rearrange("a q t -> q a t").bitcast(I32)
             )
-        nc.sync.dma_start(wgt_rows[0:64, :], wgt2[0:P:16, :].rearrange("g (e j) -> g e j", e=8))
+        nc.sync.dma_start(wgt_rows[0 : P // 2, :], wgt2[0:P:16, :].rearrange("g (e j) -> g e j", e=J // P))
         nc.sync.dma_start(tab_w[:], tab_words[0].rearrange("p t b -> p (t b)").bitcast(I32))
         nc.sync.dma_start(idx2[:], offs2)
         wa_rows = wa.rearrange("(p i) r -> p i r", i=PACK)
@@ -92,18 +96,17 @@ def tile_list_htabg_glu_biasP_kernel(
         nc.sync.dma_start(planes[0][:], x_rows[0])
         for q in range(4):
             nc.sync.dma_start(
-                ws[32 * q : 32 * q + 4, :, :].bitcast(I32),
+                wb_s[32 * q : 32 * q + 4, :, :].bitcast(I32),
                 wb_scales[:, 4 * q : 4 * q + 4, :].rearrange("a r c -> r a c").bitcast(I32),
             )
         nc.sync.dma_start(wa_raw[1][:], wa_rows[:, :, R // 2 : R])
         nc.vector.tensor_copy(got_s[:], tab_s[:].indirect(idx[:]))
         nc.sync.dma_start(got_s1[0:100, :].bitcast(I32), got_s[16:116, :].bitcast(I32))
-        nc.sync.dma_start(planes[1][:], x_rows[1])
-        nc.sync.dma_start(planes[2][:], x_rows[2])
-        nc.sync.dma_start(planes[3][:], x_rows[3])
+        for i in range(1, PACK):
+            nc.sync.dma_start(planes[i][:], x_rows[i])
         for q in range(4):
             nc.sync.dma_start(
-                ds_raw[32 * q : 32 * q + 4, :].bitcast(I32), wd_scales[0, 4 * q : 4 * q + 4, :].bitcast(I32)
+                wd_s_raw[32 * q : 32 * q + 4, :].bitcast(I32), wd_scales[0, 4 * q : 4 * q + 4, :].bitcast(I32)
             )
         nc.sync.dma_start(wd_raw[:], wd_words[0].rearrange("p n b -> p (n b)").bitcast(I32))
         nc.sync.dma_start(bias[:], b.rearrange("(p t) -> p t", t=PACK))
@@ -112,7 +115,7 @@ def tile_list_htabg_glu_biasP_kernel(
         nc.tensor.transpose(turned[:], wgt_rows[:], ident[:])
         nc.scalar.copy(
             wgt_wide[:].rearrange("p e (g d) -> p e g d", d=16),
-            turned[:, 0:64].rearrange("p (g e) -> p e g", e=8).unsqueeze(3).to_broadcast([P, 8, 8, 16]),
+            turned[:, 0 : P // 2].rearrange("p (g e) -> p e g", g=HEADS).unsqueeze(3).to_broadcast([P, J // P, HEADS, 16]),
         )
         for u in range(2):
             back = psum.tile([P, PACK, P], F32, name="bank")
@@ -120,50 +123,47 @@ def tile_list_htabg_glu_biasP_kernel(
                 nc.tensor.transpose(back[:, e, :], wgt_wide[:, PACK * u + e, :], ident[:])
             nc.scalar.copy(wgt[:, u * HALF : (u + 1) * HALF], back[:].rearrange("p e j -> p (e j)"))
 
-
-        early = keep.tile([P, 22, CH], F32, align_bytes=64)
-        x_q = [ring.tile([P, CH], U32, name="x_q", align_bytes=64) for g in range(NG)]
-        x_s = [ring.tile([P, CH], U8, name="x_s", align_bytes=64) for g in range(NG)]
-        x_bf = [ring.tile([P, CH, PACK], BF16, name="x_bf", align_bytes=64) for g in range(NG)]
-        t_q = keep.tile([P, 2, 2 * J], U8, align_bytes=64)
+        picks = keep.tile([P, PLACES, GROUP], F32, align_bytes=64)
+        x_q = [ring.tile([P, GROUP], U32, name="x_q", align_bytes=64) for g in range(GROUPS)]
+        x_s = [ring.tile([P, GROUP], U8, name="x_s", align_bytes=64) for g in range(GROUPS)]
+        x_bf = [ring.tile([P, GROUP, PACK], BF16, name="x_bf", align_bytes=64) for g in range(GROUPS)]
+        tab_q = keep.tile([P, 2, 2 * J], U8, align_bytes=64)
         got_w = keep.tile([P, J], U32, align_bytes=64)
         h_bf = [ring.tile([P, w, PACK], BF16, name="h_bf", align_bytes=64) for w in WIDTHS]
         h_q = [ring.tile([P, w], U32, name="h_q", align_bytes=64) for w in WIDTHS]
         h_s = [ring.tile([P, w], U8, name="h_s", align_bytes=64) for w in WIDTHS]
         y_q = keep.tile([P, J], I32, align_bytes=64)
         act = [ring.tile([P, w, PACK], F32, name="act", align_bytes=64) for w in WIDTHS]
-        yb_last = keep.tile([P, 6, R], F32, align_bytes=64)
+        yb_rest = keep.tile([P, J // SUB - 2, R], F32, align_bytes=64)
         wa_place = wa_raw[1][:].rearrange("p (s i) r -> p s (i r)", s=2)
-        yb_t = [wa_place[:, s, :] for s in range(2)] + [yb_last[:, s, :] for s in range(6)]
+        yb_t = [wa_place[:, s, :] for s in range(2)] + [yb_rest[:, s, :] for s in range(J // SUB - 2)]
         y_sb = keep.tile([P, PACK, J], F32, align_bytes=64)
         y_bf = keep.tile([P, J, PACK], BF16, align_bytes=64)
+        out_rows = out_0.rearrange("(p t) j -> p t j", t=PACK)
 
-        def cols(c):
-            return slice(STARTS[c], STARTS[c] + WIDTHS[c])
-
-        def entries(lst, j0, n):
-            return lst[:, j0 // 16 : (j0 + n) // 16]
-
-        def interleave(copy, dst, src):
-            copy(dst.rearrange("p (c i) t -> p c t i", i=4), src.rearrange("p t (c i) -> p c t i", i=4))
+        def cols(c0, c1):
+            return slice(STARTS[c0], STARTS[c1] + WIDTHS[c1])
 
         def quantize(codes, scales, src):
             nc.vector.quantize_mx(out=codes.bitcast(FP8X4), scales=scales, in_=src)
 
-        def pick_x(dst, i, j0, n):
-            nc.vector.tensor_tensor(dst, planes[i][:].indirect(entries(idx2, j0, n)), wgt[:, j0 : j0 + n], MULT)
-
-        def pick_late(i, g, n):
-            first = LATE[g] + 4 * (i - 2)
-            pick_x(early[:, first : first + n, :].rearrange("p s c -> p (s c)"), i, g * CH, n * CH)
+        def pick(i, place, g, n):
+            tokens = slice(g * GROUP, (g + n) * GROUP)
+            nc.vector.tensor_tensor(
+                picks[:, place : place + n, :].rearrange("p s c -> p (s c)"),
+                planes[i][:].indirect(idx2[:, tokens.start // 16 : tokens.stop // 16]), wgt[:, tokens], MULT,
+            )
 
         def round_x(g):
             step = LATE[g] - g
-            src = early[:, g : g + 2 * step, :].rearrange("p (a x) c -> p a x c", a=2)[:, :, 0:5:4, :]
+            src = picks[:, g : g + 2 * step, :].rearrange("p (a x) c -> p a x c", a=2)[:, :, 0 : PACK + 1 : PACK, :]
             nc.scalar.copy(
                 x_bf[g][:].rearrange("p (c i) (a e) -> p c a e i", i=4, a=2),
                 src.rearrange("p a e (c i) -> p c a e i", i=4),
             )
+
+        def quant_x(g):
+            quantize(x_q[g][:], x_s[g][:], x_bf[g][:].rearrange("p c t -> p (c t)"))
 
         def deal_wd():
             nc.vector.tensor_copy(
@@ -171,25 +171,25 @@ def tile_list_htabg_glu_biasP_kernel(
                 wd_raw[:].rearrange("p (m i t) -> p m t i", t=PACK, i=4),
             )
             nc.vector.tensor_copy(
-                ds[:].rearrange("p (t m) -> p t m", t=PACK), ds_raw[:].rearrange("p (m t) -> p t m", t=PACK)
+                wd_s[:].rearrange("p (t m) -> p t m", t=PACK), wd_s_raw[:].rearrange("p (m t) -> p t m", t=PACK)
             )
 
-        def quant_x(g):
-            quantize(x_q[g][:], x_s[g][:], x_bf[g][:].rearrange("p c t -> p (c t)"))
-
         def memory(s):
-            yb = psum.tile([P, R], F32, name="bank") if s < 5 else psum_yb.tile([P, R], F32, name="yb_bank")
+            if s < 8 - YB_BANKS:
+                yb = psum.tile([P, R], F32, name="bank")
+            else:
+                yb = psum_yb.tile([P, R], F32, name="yb_bank")
             j0 = s * SUB
             for a in range(2):
                 nc.tensor.matmul_mx(
-                    out=yb[:], lhsT=t_q[:, a, 2 * j0 : 2 * (j0 + SUB)].bitcast(FP4X4),
+                    out=yb[:], lhsT=tab_q[:, a, 2 * j0 : 2 * (j0 + SUB)].bitcast(FP4X4),
                     lhsT_scale=(got_s, got_s1)[a][:, j0 : j0 + SUB],
-                    rhs=wb_q[:, a, :].bitcast(FP4X4), rhs_scale=ws[:, a, :], start=(a == 0), stop=(a == 1),
+                    rhs=wb_q[:, a, :].bitcast(FP4X4), rhs_scale=wb_s[:, a, :], start=(a == 0), stop=(a == 1),
                 )
             nc.scalar.copy(yb_t[s].rearrange("p (t m) -> p t m", t=PACK), yb[:].rearrange("p (m t) -> p t m", t=PACK))
 
-        def gate(g, subs=(0, 1)):
-            for s in subs:
+        def gate(g):
+            for s in range(GROUP // SUB):
                 sub = slice(s * SUB, (s + 1) * SUB)
                 ya = psum.tile([P, PACK, SUB], F32, name="bank")
                 for t in range(PACK):
@@ -198,7 +198,7 @@ def tile_list_htabg_glu_biasP_kernel(
                         out=ya[:, t, :], lhsT=wa_q[:, m].bitcast(FP8X4), lhsT_scale=wa_s[:, m],
                         rhs=x_q[g][:, sub].bitcast(FP8X4), rhs_scale=x_s[g][:, sub], start=True, stop=True,
                     )
-                dst = act[g][:, sub, :] if g < 3 else act[3 + s][:]
+                dst = act[g][:, sub, :] if WIDTHS[g] == GROUP else act[g + s][:]
                 nc.scalar.activation(dst, ya[:].rearrange("p t n -> p n t"), ACT.Silu)
 
         def join(c):
@@ -212,54 +212,51 @@ def tile_list_htabg_glu_biasP_kernel(
         def quant_h(c):
             quantize(h_q[c][:], h_s[c][:], h_bf[c][:].rearrange("p c t -> p (c t)"))
 
+        def project(out, t, c):
+            m = slice(t * P, (t + 1) * P)
+            nc.tensor.matmul_mx(
+                out=out, lhsT=wd_q[:, m].bitcast(FP8X4), lhsT_scale=wd_s[:, m],
+                rhs=h_q[c][:].bitcast(FP8X4), rhs_scale=h_s[c][:], start=True, stop=True,
+            )
+
         def down(c):
-            w = WIDTHS[c]
-            per_bank = 512 // w
+            per_bank = BANK // WIDTHS[c]
             for t0 in range(0, PACK, per_bank):
-                y = psum.tile([P, per_bank, w], F32, name="bank")
+                y = psum.tile([P, per_bank, WIDTHS[c]], F32, name="bank")
                 for e in range(per_bank):
-                    m = slice((t0 + e) * P, (t0 + e + 1) * P)
-                    nc.tensor.matmul_mx(
-                        out=y[:, e, :], lhsT=wd_q[:, m].bitcast(FP8X4), lhsT_scale=ds[:, m],
-                        rhs=h_q[c][:].bitcast(FP8X4), rhs_scale=h_s[c][:], start=True, stop=True,
-                    )
+                    project(y[:, e, :], t0 + e, c)
                 for e in range(per_bank):
                     t = t0 + e
-                    nc.scalar.activation(y_sb[:, t, cols(c)], y[:, e, :], ACT.Identity, bias=bias[:, t : t + 1])
-                if per_bank < PACK:
-                    rows = slice(t0, t0 + per_bank)
-                    nc.sync.dma_start(out_0.rearrange("(p t) j -> p t j", t=PACK)[:, rows, cols(c)], y_sb[:, rows, cols(c)])
+                    nc.scalar.activation(y_sb[:, t, cols(c, c)], y[:, e, :], ACT.Identity, bias=bias[:, t : t + 1])
+                rows = slice(t0, t0 + per_bank)
+                nc.sync.dma_start(out_rows[:, rows, cols(c, c)], y_sb[:, rows, cols(c, c)])
+
+        def round_y(copy, c):
+            copy(
+                y_bf[:, cols(c, c), :].rearrange("p (c i) t -> p c t i", i=4),
+                y_sb[:, :, cols(c, c)].rearrange("p t (c i) -> p c t i", i=4),
+            )
 
         def round_from_sums(c):
             y = psum.tile([P, PACK, SUB], F32, name="bank")
             for t in range(PACK):
-                m = slice(t * P, (t + 1) * P)
-                nc.tensor.matmul_mx(
-                    out=y[:, t, :], lhsT=wd_q[:, m].bitcast(FP8X4), lhsT_scale=ds[:, m],
-                    rhs=h_q[c][:].bitcast(FP8X4), rhs_scale=h_s[c][:], start=True, stop=True,
-                )
+                project(y[:, t, :], t, c)
             nc.vector.tensor_tensor(
-                y_bf[:, cols(c), :], y[:].rearrange("p t n -> p n t"),
+                y_bf[:, cols(c, c), :], y[:].rearrange("p t n -> p n t"),
                 bias[:].unsqueeze(1).to_broadcast([P, SUB, PACK]), ADD,
             )
 
-        def store_y(j0, j1):
-            nc.sync.dma_start(out_0.rearrange("(p t) j -> p t j", t=PACK)[:, :, j0:j1], y_sb[:, :, j0:j1])
+        def quant_y(c0, c1):
+            quantize(y_q[:, cols(c0, c1)], out_s[:, cols(c0, c1)], y_bf[:, cols(c0, c1), :].rearrange("p c t -> p (c t)"))
 
-        def round_y(copy, j0, j1):
-            interleave(copy, y_bf[:, j0:j1, :], y_sb[:, :, j0:j1])
-
-        def quant_y(j0, j1):
-            quantize(y_q[:, j0:j1], out_s[:, j0:j1], y_bf[:, j0:j1, :].rearrange("p c t -> p (c t)"))
-
-        def store_codes(j0, j1):
-            nc.sync.dma_start(out_1[0].rearrange("p j b -> p (j b)").bitcast(I32)[:, j0:j1], y_q[:, j0:j1])
+        def store_codes(c0, c1):
+            nc.sync.dma_start(out_1[0].rearrange("p j b -> p (j b)").bitcast(I32)[:, cols(c0, c1)], y_q[:, cols(c0, c1)])
 
         nc.vector.tensor_copy(got_w[:], tab_w[:].bitcast(U32).indirect(idx[:]))
         for u in range(2):
             half = slice(u * HALF, (u + 1) * HALF)
             nc.vector.tensor_copy(
-                t_q[:].bitcast(U16)[:, :, half], got_w[:, half].bitcast(U16).rearrange("p (j d) -> p d j", d=2)
+                tab_q[:].bitcast(U16)[:, :, half], got_w[:, half].bitcast(U16).rearrange("p (j d) -> p d j", d=2)
             )
         for u in range(2):
             nc.scalar.copy(
@@ -270,56 +267,42 @@ def tile_list_htabg_glu_biasP_kernel(
         for s in range(J // SUB):
             memory(s)
         for i in range(2):
-            pick_x(early[:, 4 * i : 4 * i + 4, :].rearrange("p s c -> p (s c)"), i, 0, J)
-        pick_late(2, 0, 3)
-        pick_late(3, 0, 1)
-        round_x(0)
-        pick_late(3, 1, 1)
-        round_x(1)
-        quant_x(0)
-        gate(0)
-        pick_late(3, 2, 1)
-        quant_x(1)
-        round_x(2)
-        gate(1)
-        pick_late(2, 3, 1)
-        pick_late(3, 3, 1)
-        deal_wd()
-        join(0)
-        quant_x(2)
-        quant_h(0)
-        round_x(3)
-        join(1)
-        gate(2)
-        quant_x(3)
-        quant_h(1)
-        down(0)
-        gate(3)
-        join(2)
-        quant_h(2)
-        down(1)
-        join(3)
-        join(4)
-        quant_h(3)
-        quant_h(4)
-        down(2)
-        round_y(nc.vector.tensor_copy, 0, 256)
-        quant_y(0, 256)
-        store_codes(0, 256)
-        round_y(nc.vector.tensor_copy, 256, 512)
-        down(3)
-        store_y(768, 896)
-        quant_y(256, 512)
-        down(4)
-        store_y(896, 1024)
-        round_y(nc.vector.tensor_copy, 512, 768)
-        quant_y(512, 768)
-        store_codes(256, 768)
-        round_y(nc.vector.tensor_copy, 768, 896)
-        quant_y(768, 896)
-        round_from_sums(4)
-        quant_y(896, 1024)
-        store_codes(768, 1024)
+            pick(i, GROUPS * i, 0, GROUPS)
+        pick(2, LATE[0], 0, GROUPS - 1)
+
+        def chunks_of(g):
+            return [c for c in range(CHUNKS) if STARTS[c] // GROUP == g]
+
+        last = GROUPS - 1
+        for k in range(GROUPS + 4):
+            if k == last:
+                pick(2, LATE[k], k, 1)
+            if k <= last:
+                pick(3, LATE[k] + PACK, k, 1)
+                round_x(k)
+            if k == 3:
+                deal_wd()
+            for c in chunks_of(k - 3):
+                join(c)
+            if 0 <= k - 1 <= last:
+                quant_x(k - 1)
+            for c in chunks_of(k - 3):
+                quant_h(c)
+            for c in chunks_of(k - 4):
+                down(c)
+            if 0 <= k - 1 <= last:
+                gate(k - 1)
+
+        for c in range(CHUNKS - 2):
+            round_y(nc.vector.tensor_copy, c)
+            quant_y(c, c)
+            if c == 0:
+                store_codes(0, 0)
+        store_codes(1, CHUNKS - 3)
+        round_y(nc.scalar.copy, CHUNKS - 2)
+        round_from_sums(CHUNKS - 1)
+        quant_y(CHUNKS - 2, CHUNKS - 1)
+        store_codes(CHUNKS - 2, CHUNKS - 1)
         for q in range(4):
             queue = nc.scalar if q % 2 else nc.sync
             queue.dma_start(out_2[0, 4 * q : 4 * q + 4, :].bitcast(I32), out_s[32 * q : 32 * q + 4, :].bitcast(I32))

@@ -175,10 +175,7 @@ def tile_list_htabg_glu_biasP_kernel(
             )
 
         def memory(s):
-            if s < 8 - YB_BANKS:
-                yb = psum.tile([P, R], F32, name="bank")
-            else:
-                yb = psum_yb.tile([P, R], F32, name="yb_bank")
+            yb = early[s % YB_BANKS]
             j0 = s * SUB
             for a in range(2):
                 nc.tensor.matmul_mx(
@@ -264,6 +261,7 @@ def tile_list_htabg_glu_biasP_kernel(
                 wa_raw[u][:].rearrange("p i (m t) -> p m i t", t=PACK),
             )
         quantize(wa_q[:], wa_s[:], wa_bf[:])
+        early = [psum_yb.tile([P, R], F32, name="yb_bank") for e in range(YB_BANKS)]
         for s in range(J // SUB):
             memory(s)
         for i in range(2):

@@ -99,17 +99,17 @@ def tile_list_htabg_glu_biasP_kernel(
                 wb_s[32 * q : 32 * q + 4, :, :].bitcast(I32),
                 wb_scales[:, 4 * q : 4 * q + 4, :].rearrange("a r c -> r a c").bitcast(I32),
             )
-        nc.sync.dma_start(wa_raw[1][:], wa_rows[:, :, R // 2 : R])
+        nc.sync.dma_start(bias[:], b.rearrange("(p t) -> p t", t=PACK))
         nc.vector.tensor_copy(got_s[:], tab_s[:].indirect(idx[:]))
         nc.sync.dma_start(got_s1[0:100, :].bitcast(I32), got_s[16:116, :].bitcast(I32))
         for i in range(1, PACK):
             nc.sync.dma_start(planes[i][:], x_rows[i])
+        nc.sync.dma_start(wa_raw[1][:], wa_rows[:, :, R // 2 : R])
+        nc.sync.dma_start(wd_raw[:], wd_words[0].rearrange("p n b -> p (n b)").bitcast(I32))
         for q in range(4):
             nc.sync.dma_start(
                 wd_s_raw[32 * q : 32 * q + 4, :].bitcast(I32), wd_scales[0, 4 * q : 4 * q + 4, :].bitcast(I32)
             )
-        nc.sync.dma_start(wd_raw[:], wd_words[0].rearrange("p n b -> p (n b)").bitcast(I32))
-        nc.sync.dma_start(bias[:], b.rearrange("(p t) -> p t", t=PACK))
 
         turned = psum.tile([P, P], F32, name="bank")
         nc.tensor.transpose(turned[:], wgt_rows[:], ident[:])
@@ -134,9 +134,8 @@ def tile_list_htabg_glu_biasP_kernel(
         h_s = [ring.tile([P, w], U8, name="h_s", align_bytes=64) for w in WIDTHS]
         y_q = keep.tile([P, J], I32, align_bytes=64)
         act = [ring.tile([P, w, PACK], F32, name="act", align_bytes=64) for w in WIDTHS]
-        yb_rest = keep.tile([P, J // SUB - 2, R], F32, align_bytes=64)
-        wa_place = wa_raw[1][:].rearrange("p (s i) r -> p s (i r)", s=2)
-        yb_t = [wa_place[:, s, :] for s in range(2)] + [yb_rest[:, s, :] for s in range(J // SUB - 2)]
+        yb_all = keep.tile([P, J // SUB, R], F32, align_bytes=64)
+        yb_t = [yb_all[:, s, :] for s in range(J // SUB)]
         y_sb = keep.tile([P, PACK, J], F32, align_bytes=64)
         y_bf = keep.tile([P, J, PACK], BF16, align_bytes=64)
         out_rows = out_0.rearrange("(p t) j -> p t j", t=PACK)
@@ -255,11 +254,11 @@ def tile_list_htabg_glu_biasP_kernel(
             nc.vector.tensor_copy(
                 tab_q[:].bitcast(U16)[:, :, half], got_w[:, half].bitcast(U16).rearrange("p (j d) -> p d j", d=2)
             )
-        for u in range(2):
-            nc.scalar.copy(
-                wa_bf[:].rearrange("p (t u m i) -> p u m i t", t=PACK, u=2, i=PACK)[:, u],
-                wa_raw[u][:].rearrange("p i (m t) -> p m i t", t=PACK),
-            )
+        wa_dealt = wa_bf[:].rearrange("p (t m i) -> p m i t", t=PACK, i=PACK)
+        wa_half = [wa_raw[u][:].rearrange("p i (m t) -> p m i t", t=PACK) for u in range(2)]
+        nc.scalar.copy(wa_dealt[:, 0 : P // 2], wa_half[0])
+        nc.scalar.copy(wa_dealt[:, P // 2 : 3 * P // 4], wa_half[1][:, 0 : P // 4])
+        nc.vector.tensor_copy(wa_dealt[:, 3 * P // 4 : P], wa_half[1][:, P // 4 : P // 2])
         quantize(wa_q[:], wa_s[:], wa_bf[:])
         early = [psum_yb.tile([P, R], F32, name="yb_bank") for e in range(YB_BANKS)]
         for s in range(J // SUB):

@@ -51,7 +51,7 @@ def tile_list_htabg_glu_biasP_kernel(
         tab_w = keep.tile([P, T], I32, align_bytes=64)
         tab_s = keep.tile([P, T], U8, align_bytes=64)
         got_s = keep.tile([P, J], U8, align_bytes=64)
-        got_s1 = keep.tile([P, J], U8, align_bytes=64)
+        tab_planes = keep.tile([P, 2, J], U8, align_bytes=64)
         planes = [keep.tile([P, T], F32, name="x_plane%d" % i, align_bytes=64) for i in range(PACK)]
         wgt = keep.tile([P, J], F32, align_bytes=64)
         wgt_rows = keep.tile([P, P], F32, align_bytes=64)
@@ -72,36 +72,35 @@ def tile_list_htabg_glu_biasP_kernel(
         warm = keep.tile([P, 1], F32, align_bytes=64)
         out_s = keep.tile([P, J], U8, align_bytes=64)
 
-        nc.gpsimd.memset(tab_s[:].bitcast(I32), 0)
+        nc.gpsimd.memset(tab_s[0:96, :].bitcast(I32), 0)
         nc.vector.memset(zero[:], 0.0)
         nc.scalar.activation(warm[:], zero[:], ACT.Silu)
         nc.gpsimd.memset(wgt_rows[P // 2 : P, :], 0.0)
         make_identity(nc, ident[:])
-        nc.gpsimd.memset(wb_s[:].rearrange("p a r -> p (a r)").bitcast(I32), 0)
-        nc.gpsimd.memset(wd_s_raw[:].bitcast(I32), 0)
-        nc.gpsimd.memset(got_s1[:].bitcast(I32), 0)
+        nc.vector.memset(wb_s[:].rearrange("p a r -> p (a r)").bitcast(I32), 0)
+        nc.vector.memset(tab_planes[:].rearrange("p a j -> p (a j)").bitcast(I32), 0)
+        nc.vector.memset(wd_s_raw[:].bitcast(I32), 0)
 
         x_rows = xT.rearrange("(p i) t -> i p t", i=PACK)
         nc.sync.dma_start(idx[:], offs)
-        nc.sync.dma_start(wb_q[:].bitcast(I32), wb_words.rearrange("a p c -> p a c").bitcast(I32))
-        for r in range(4):
-            nc.sync.dma_start(
-                tab_s[r:P:16, :].bitcast(I32), tab_scales[:, r:16:4, :].rearrange("a q t -> q a t").bitcast(I32)
-            )
+        nc.sync.dma_start(tab_s[96:P, :].bitcast(I32), tab_scales.rearrange("a x t -> x a t").bitcast(I32))
         nc.sync.dma_start(wgt_rows[0 : P // 2, :], wgt2[0:P:16, :].rearrange("g (e j) -> g e j", e=J // P))
         nc.sync.dma_start(tab_w[:], tab_words[0].rearrange("p t b -> p (t b)").bitcast(I32))
         nc.sync.dma_start(idx2[:], offs2)
-        wa_rows = wa.rearrange("(p i) r -> p i r", i=PACK)
-        nc.sync.dma_start(wa_raw[0][:], wa_rows[:, :, 0 : R // 2])
-        nc.sync.dma_start(planes[0][:], x_rows[0])
         for q in range(4):
             nc.sync.dma_start(
                 wb_s[32 * q : 32 * q + 4, :, :].bitcast(I32),
                 wb_scales[:, 4 * q : 4 * q + 4, :].rearrange("a r c -> r a c").bitcast(I32),
             )
-        nc.sync.dma_start(bias[:], b.rearrange("(p t) -> p t", t=PACK))
+        nc.sync.dma_start(wb_q[:].bitcast(I32), wb_words.rearrange("a p c -> p a c").bitcast(I32))
+        nc.sync.dma_start(planes[0][:], x_rows[0])
+        wa_rows = wa.rearrange("(p i) r -> p i r", i=PACK)
+        nc.sync.dma_start(wa_raw[0][:], wa_rows[:, :, 0 : R // 2])
         nc.vector.tensor_copy(got_s[:], tab_s[:].indirect(idx[:]))
-        nc.sync.dma_start(got_s1[0:100, :].bitcast(I32), got_s[16:116, :].bitcast(I32))
+        for q in range(4):
+            nc.sync.dma_start(
+                tab_planes[32 * q : 32 * q + 4, :, :].bitcast(I32), got_s[96 + 8 * q : 104 + 8 * q, :].bitcast(I32)
+            )
         for i in range(1, PACK):
             nc.sync.dma_start(planes[i][:], x_rows[i])
         nc.sync.dma_start(wa_raw[1][:], wa_rows[:, :, R // 2 : R])
@@ -110,6 +109,7 @@ def tile_list_htabg_glu_biasP_kernel(
             nc.sync.dma_start(
                 wd_s_raw[32 * q : 32 * q + 4, :].bitcast(I32), wd_scales[0, 4 * q : 4 * q + 4, :].bitcast(I32)
             )
+        nc.sync.dma_start(bias[:], b.rearrange("(p t) -> p t", t=PACK))
 
         turned = psum.tile([P, P], F32, name="bank")
         nc.tensor.transpose(turned[:], wgt_rows[:], ident[:])
@@ -179,7 +179,7 @@ def tile_list_htabg_glu_biasP_kernel(
             for a in range(2):
                 nc.tensor.matmul_mx(
                     out=yb[:], lhsT=tab_q[:, a, 2 * j0 : 2 * (j0 + SUB)].bitcast(FP4X4),
-                    lhsT_scale=(got_s, got_s1)[a][:, j0 : j0 + SUB],
+                    lhsT_scale=tab_planes[:, a, j0 : j0 + SUB],
                     rhs=wb_q[:, a, :].bitcast(FP4X4), rhs_scale=wb_s[:, a, :], start=(a == 0), stop=(a == 1),
                 )
             nc.scalar.copy(yb_t[s].rearrange("p (t m) -> p t m", t=PACK), yb[:].rearrange("p (m t) -> p t m", t=PACK))

@@ -87,28 +87,26 @@ def tile_list_htabg_glu_biasP_kernel(
         nc.sync.dma_start(wgt_rows[0 : P // 2, :], wgt2[0:P:16, :].rearrange("g (e j) -> g e j", e=J // P))
         nc.sync.dma_start(tab_w[:], tab_words[0].rearrange("p t b -> p (t b)").bitcast(I32))
         nc.sync.dma_start(idx2[:], offs2)
-        for q in range(4):
+        for r in range(4):
             nc.sync.dma_start(
-                wb_s[32 * q : 32 * q + 4, :, :].bitcast(I32),
-                wb_scales[:, 4 * q : 4 * q + 4, :].rearrange("a r c -> r a c").bitcast(I32),
+                wb_s[r:P:32, :, :].bitcast(I32), wb_scales[:, r:16:4, :].rearrange("a q c -> q a c").bitcast(I32)
             )
-        nc.sync.dma_start(wb_q[:].bitcast(I32), wb_words.rearrange("a p c -> p a c").bitcast(I32))
         nc.sync.dma_start(planes[0][:], x_rows[0])
-        wa_rows = wa.rearrange("(p i) r -> p i r", i=PACK)
-        nc.sync.dma_start(wa_raw[0][:], wa_rows[:, :, 0 : R // 2])
+        nc.sync.dma_start(wb_q[:].bitcast(I32), wb_words.rearrange("a p c -> p a c").bitcast(I32))
         nc.vector.tensor_copy(got_s[:], tab_s[:].indirect(idx[:]))
-        for q in range(4):
+        for q in (0, 2, 1, 3):
             nc.sync.dma_start(
                 tab_planes[32 * q : 32 * q + 4, :, :].bitcast(I32), got_s[96 + 8 * q : 104 + 8 * q, :].bitcast(I32)
             )
-        for i in range(1, PACK):
+        nc.sync.dma_start(planes[1][:], x_rows[1])
+        wa_rows = wa.rearrange("(p i) r -> p i r", i=PACK)
+        nc.sync.dma_start(wa_raw[0][:], wa_rows[:, :, 0 : R // 2])
+        for i in range(2, PACK):
             nc.sync.dma_start(planes[i][:], x_rows[i])
         nc.sync.dma_start(wa_raw[1][:], wa_rows[:, :, R // 2 : R])
         nc.sync.dma_start(wd_raw[:], wd_words[0].rearrange("p n b -> p (n b)").bitcast(I32))
-        for q in range(4):
-            nc.sync.dma_start(
-                wd_s_raw[32 * q : 32 * q + 4, :].bitcast(I32), wd_scales[0, 4 * q : 4 * q + 4, :].bitcast(I32)
-            )
+        for r in range(4):
+            nc.sync.dma_start(wd_s_raw[r:P:32, :].bitcast(I32), wd_scales[0, r:16:4, :].bitcast(I32))
         nc.sync.dma_start(bias[:], b.rearrange("(p t) -> p t", t=PACK))
 
         turned = psum.tile([P, P], F32, name="bank")
@@ -300,6 +298,6 @@ def tile_list_htabg_glu_biasP_kernel(
         round_from_sums(CHUNKS - 1)
         quant_y(CHUNKS - 2, CHUNKS - 1)
         store_codes(CHUNKS - 2, CHUNKS - 1)
-        for q in range(4):
-            queue = nc.scalar if q % 2 else nc.sync
-            queue.dma_start(out_2[0, 4 * q : 4 * q + 4, :].bitcast(I32), out_s[32 * q : 32 * q + 4, :].bitcast(I32))
+        for r in range(4):
+            queue = nc.scalar if r % 2 else nc.sync
+            queue.dma_start(out_2[0, r:16:4, :].bitcast(I32), out_s[r:P:32, :].bitcast(I32))

@@ -43,6 +43,7 @@ def tile_list_htabg_glu_biasP_kernel(
         lists = ctx.enter_context(tc.tile_pool(name="lists", bufs=1))
         keep = ctx.enter_context(tc.tile_pool(name="keep", bufs=1))
         ring = ctx.enter_context(tc.tile_pool(name="ring", bufs=CHUNKS))
+        over = ctx.enter_context(tc.tile_pool(name="over", bufs=1))
         psum = ctx.enter_context(tc.psum_pool(name="psum", bufs=8 - YB_BANKS))
         psum_yb = ctx.enter_context(tc.psum_pool(name="psum_yb", bufs=YB_BANKS))
 
@@ -127,15 +128,18 @@ def tile_list_htabg_glu_biasP_kernel(
         x_bf = [ring.tile([P, GROUP, PACK], BF16, name="x_bf", align_bytes=64) for g in range(GROUPS)]
         tab_q = keep.tile([P, 2, 2 * J], U8, align_bytes=64)
         got_w = keep.tile([P, J], U32, align_bytes=64)
-        h_bf = [ring.tile([P, w, PACK], BF16, name="h_bf", align_bytes=64) for w in WIDTHS]
-        h_q = [ring.tile([P, w], U32, name="h_q", align_bytes=64) for w in WIDTHS]
+        h_bf = [ring.tile([P, w, PACK], BF16, name="h_bf", align_bytes=64) for w in WIDTHS[:-1]]
+        h_bf += [over.tile([P, WIDTHS[-1], PACK], BF16, name="h_bf_last", align_bytes=64, offset=4096)]
+        y_bf0 = over.tile([P, WIDTHS[0], PACK], BF16, align_bytes=64, offset=4096)
+        h_q = [over.tile([P, w], U32, name="h_q1", align_bytes=64, offset=0) if c == 1 else ring.tile([P, w], U32, name="h_q", align_bytes=64) for c, w in enumerate(WIDTHS)]
         h_s = [ring.tile([P, w], U8, name="h_s", align_bytes=64) for w in WIDTHS]
         y_q = keep.tile([P, J], I32, align_bytes=64)
-        act = [ring.tile([P, w, PACK], F32, name="act", align_bytes=64) for w in WIDTHS]
+        act = [ring.tile([P, w, PACK], F32, name="act", align_bytes=64) for w in WIDTHS[:-1]]
+        act += [over.tile([P, WIDTHS[-1], PACK], F32, name="act_last", align_bytes=64, offset=0)]
         yb_all = keep.tile([P, J // SUB, R], F32, align_bytes=64)
         yb_t = [yb_all[:, s, :] for s in range(J // SUB)]
         y_sb = keep.tile([P, PACK, J], F32, align_bytes=64)
-        y_bf = keep.tile([P, J, PACK], BF16, align_bytes=64)
+        y_bf = over.tile([P, J, PACK], BF16, align_bytes=64, offset=4096)
         out_rows = out_0.rearrange("(p t) j -> p t j", t=PACK)
 
         def cols(c0, c1):
@@ -182,8 +186,8 @@ def tile_list_htabg_glu_biasP_kernel(
                 )
             nc.scalar.copy(yb_t[s].rearrange("p (t m) -> p t m", t=PACK), yb[:].rearrange("p (m t) -> p t m", t=PACK))
 
-        def gate(g):
-            for s in range(GROUP // SUB):
+        def gate(g, blocks):
+            for s in blocks:
                 sub = slice(s * SUB, (s + 1) * SUB)
                 ya = psum.tile([P, PACK, SUB], F32, name="bank")
                 for t in range(PACK):
@@ -223,12 +227,15 @@ def tile_list_htabg_glu_biasP_kernel(
                     t = t0 + e
                     nc.scalar.activation(y_sb[:, t, cols(c, c)], y[:, e, :], ACT.Identity, bias=bias[:, t : t + 1])
                 rows = slice(t0, t0 + per_bank)
-                nc.sync.dma_start(out_rows[:, rows, cols(c, c)], y_sb[:, rows, cols(c, c)])
+                if c:
+                    nc.sync.dma_start(out_rows[:, rows, cols(c, c)], y_sb[:, rows, cols(c, c)])
+            if c == 0:
+                nc.sync.dma_start(out_rows[:, :, cols(c, c)], y_sb[:, :, cols(c, c)])
 
-        def round_y(copy, c):
+        def round_y(copy, c0, c1):
             copy(
-                y_bf[:, cols(c, c), :].rearrange("p (c i) t -> p c t i", i=4),
-                y_sb[:, :, cols(c, c)].rearrange("p t (c i) -> p c t i", i=4),
+                (y_bf if c0 else y_bf0)[:, cols(c0, c1), :].rearrange("p (c i) t -> p c t i", i=4),
+                y_sb[:, :, cols(c0, c1)].rearrange("p t (c i) -> p c t i", i=4),
             )
 
         def round_from_sums(c):
@@ -241,7 +248,7 @@ def tile_list_htabg_glu_biasP_kernel(
             )
 
         def quant_y(c0, c1):
-            quantize(y_q[:, cols(c0, c1)], out_s[:, cols(c0, c1)], y_bf[:, cols(c0, c1), :].rearrange("p c t -> p (c t)"))
+            quantize(y_q[:, cols(c0, c1)], out_s[:, cols(c0, c1)], (y_bf if c0 else y_bf0)[:, cols(c0, c1), :].rearrange("p c t -> p (c t)"))
 
         def store_codes(c0, c1):
             nc.sync.dma_start(out_1[0].rearrange("p j b -> p (j b)").bitcast(I32)[:, cols(c0, c1)], y_q[:, cols(c0, c1)])
@@ -278,26 +285,27 @@ def tile_list_htabg_glu_biasP_kernel(
             if k == 3:
                 deal_wd()
             for c in chunks_of(k - 3):
+                if c == CHUNKS - 1:
+                    quant_h(c - 1)
+                    round_y(nc.vector.tensor_copy, 0, 0)
+                    quant_y(0, 0)
+                    store_codes(0, 0)
                 join(c)
             if 0 <= k - 1 <= last:
                 quant_x(k - 1)
-            for c in chunks_of(k - 3):
+            for c in chunks_of(k - 3)[-1:]:
                 quant_h(c)
             for c in chunks_of(k - 4):
                 down(c)
             if 0 <= k - 1 <= last:
-                gate(k - 1)
+                gate(k - 1, range(GROUP // SUB if k <= last else 1))
+            if k == last + 2:
+                gate(last, [1])
 
-        for c in range(CHUNKS - 2):
-            round_y(nc.vector.tensor_copy, c)
-            quant_y(c, c)
-            if c == 0:
-                store_codes(0, 0)
-        store_codes(1, CHUNKS - 3)
-        round_y(nc.scalar.copy, CHUNKS - 2)
-        round_from_sums(CHUNKS - 1)
-        quant_y(CHUNKS - 2, CHUNKS - 1)
-        store_codes(CHUNKS - 2, CHUNKS - 1)
+        for c0, c1 in ((1, 1), (2, 3), (4, 4)):
+            round_y(nc.scalar.copy if c0 == CHUNKS - 1 else nc.vector.tensor_copy, c0, c1)
+            quant_y(c0, c1)
+            store_codes(c0, c1)
         for r in range(4):
             queue = nc.scalar if r % 2 else nc.sync
             queue.dma_start(out_2[0, r:16:4, :].bitcast(I32), out_s[r:P:32, :].bitcast(I32))

from contextlib import ExitStack

import concourse.mybir as mybir
from concourse.masks import make_identity

K, L, R, N, T, J = 512, 1024, 512, 512, 2048, 1024
FLOPS = 2 * J * (K * R + L * R + R * N)

F32 = mybir.dt.float32
BF16 = mybir.dt.bfloat16
I32 = mybir.dt.int32
U32 = mybir.dt.uint32
U16 = mybir.dt.uint16
U8 = mybir.dt.uint8
FP8X4 = mybir.dt.float8_e4m3fn_x4
FP4X4 = mybir.dt.float4_e2m1fn_x4
ACT = mybir.ActivationFunctionType
MULT = mybir.AluOpType.mult
ADD = mybir.AluOpType.add

P = 128
PACK = 4
BANK = 512
SUB = BANK // PACK
HEADS = 8
HALF = J // 2
GROUP = 256
GROUPS = J // GROUP
WIDTHS = (256, 256, 256, 128, 128)
STARTS = tuple(sum(WIDTHS[:c]) for c in range(len(WIDTHS)))
CHUNKS = len(WIDTHS)
LATE = (8, 9, 10, 9)
PLACES = 2 * max(LATE)
YB_BANKS = 3


def tile_list_htabg_glu_biasP_kernel(
    tc, tab_words, tab_scales, xT, wgt2, wa, wb_words, wb_scales, wd_words, wd_scales, b, offs, offs2,
    out_0, out_1, out_2,
):
    nc = tc.nc
    with ExitStack() as ctx:
        lists = ctx.enter_context(tc.tile_pool(name="lists", bufs=1))
        keep = ctx.enter_context(tc.tile_pool(name="keep", bufs=1))
        ring = ctx.enter_context(tc.tile_pool(name="ring", bufs=CHUNKS))
        over = ctx.enter_context(tc.tile_pool(name="over", bufs=1))
        psum = ctx.enter_context(tc.psum_pool(name="psum", bufs=8 - YB_BANKS))
        psum_yb = ctx.enter_context(tc.psum_pool(name="psum_yb", bufs=YB_BANKS))

        idx = lists.tile([P, J // 16], U16)
        idx2 = lists.tile([P, J // 16], U16)
        tab_w = keep.tile([P, T], I32, align_bytes=64)
        tab_s = keep.tile([P, T], U8, align_bytes=64)
        got_s = keep.tile([P, J], U8, align_bytes=64)
        tab_planes = keep.tile([P, 2, J], U8, align_bytes=64)
        planes = [keep.tile([P, T], F32, name="x_plane%d" % i, align_bytes=64) for i in range(PACK)]
        wgt = keep.tile([P, J], F32, align_bytes=64)
        wgt_rows = keep.tile([P, P], F32, align_bytes=64)
        wgt_wide = keep.tile([P, J // P, P], F32, align_bytes=64)
        ident = keep.tile([P, P], F32, align_bytes=64)
        wa_raw = [keep.tile([P, PACK, R // 2], F32, name="wa_raw%d" % u, align_bytes=64) for u in range(2)]
        wa_bf = keep.tile([P, R * PACK], BF16, align_bytes=64)
        wa_q = keep.tile([P, R], U32, align_bytes=64)
        wa_s = keep.tile([P, R], U8, align_bytes=64)
        wb_q = keep.tile([P, 2, 2 * R], U8, align_bytes=64)
        wd_raw = keep.tile([P, N], I32, align_bytes=64)
        wd_q = keep.tile([P, N], I32, align_bytes=64)
        wb_s = keep.tile([P, 2, R], U8, align_bytes=64)
        wd_s_raw = keep.tile([P, N], U8, align_bytes=64)
        wd_s = keep.tile([P, N], U8, align_bytes=64)
        bias = keep.tile([P, PACK], F32, align_bytes=64)
        zero = keep.tile([P, 1], F32, align_bytes=64)
        warm = keep.tile([P, 1], F32, align_bytes=64)
        out_s = keep.tile([P, J], U8, align_bytes=64)

        nc.gpsimd.memset(tab_s[0:96, :].bitcast(I32), 0)
        nc.vector.memset(zero[:], 0.0)
        nc.scalar.activation(warm[:], zero[:], ACT.Silu)
        nc.gpsimd.memset(wgt_rows[P // 2 : P, :], 0.0)
        make_identity(nc, ident[:])
        nc.vector.memset(wb_s[:].rearrange("p a r -> p (a r)").bitcast(I32), 0)
        nc.vector.memset(tab_planes[:].rearrange("p a j -> p (a j)").bitcast(I32), 0)
        nc.vector.memset(wd_s_raw[:].bitcast(I32), 0)

        x_rows = xT.rearrange("(p i) t -> i p t", i=PACK)
        nc.sync.dma_start(idx[:], offs)
        nc.sync.dma_start(tab_s[96:P, :].bitcast(I32), tab_scales.rearrange("a x t -> x a t").bitcast(I32))
        nc.sync.dma_start(wgt_rows[0 : P // 2, :], wgt2[0:P:16, :].rearrange("g (e j) -> g e j", e=J // P))
        nc.sync.dma_start(tab_w[:], tab_words[0].rearrange("p t b -> p (t b)").bitcast(I32))
        nc.sync.dma_start(idx2[:], offs2)
        for r in range(4):
            nc.sync.dma_start(
                wb_s[r:P:32, :, :].bitcast(I32), wb_scales[:, r:16:4, :].rearrange("a q c -> q a c").bitcast(I32)
            )
        nc.sync.dma_start(planes[0][:], x_rows[0])
        nc.sync.dma_start(wb_q[:].bitcast(I32), wb_words.rearrange("a p c -> p a c").bitcast(I32))
        nc.vector.tensor_copy(got_s[:], tab_s[:].indirect(idx[:]))
        for q in (0, 2, 1, 3):
            nc.sync.dma_start(
                tab_planes[32 * q : 32 * q + 4, :, :].bitcast(I32), got_s[96 + 8 * q : 104 + 8 * q, :].bitcast(I32)
            )
        nc.sync.dma_start(planes[1][:], x_rows[1])
        wa_rows = wa.rearrange("(p i) r -> p i r", i=PACK)
        nc.sync.dma_start(wa_raw[0][:], wa_rows[:, :, 0 : R // 2])
        for i in range(2, PACK):
            nc.sync.dma_start(planes[i][:], x_rows[i])
        nc.sync.dma_start(wa_raw[1][:], wa_rows[:, :, R // 2 : R])
        nc.sync.dma_start(wd_raw[:], wd_words[0].rearrange("p n b -> p (n b)").bitcast(I32))
        for r in range(4):
            nc.sync.dma_start(wd_s_raw[r:P:32, :].bitcast(I32), wd_scales[0, r:16:4, :].bitcast(I32))
        nc.sync.dma_start(bias[:], b.rearrange("(p t) -> p t", t=PACK))

        turned = psum.tile([P, P], F32, name="bank")
        nc.tensor.transpose(turned[:], wgt_rows[:], ident[:])
        nc.scalar.copy(
            wgt_wide[:].rearrange("p e (g d) -> p e g d", d=16),
            turned[:, 0 : P // 2].rearrange("p (g e) -> p e g", g=HEADS).unsqueeze(3).to_broadcast([P, J // P, HEADS, 16]),
        )
        for u in range(2):
            back = psum.tile([P, PACK, P], F32, name="bank")
            for e in range(PACK):
                nc.tensor.transpose(back[:, e, :], wgt_wide[:, PACK * u + e, :], ident[:])
            nc.scalar.copy(wgt[:, u * HALF : (u + 1) * HALF], back[:].rearrange("p e j -> p (e j)"))

        picks = keep.tile([P, PLACES, GROUP], F32, align_bytes=64)
        x_q = [ring.tile([P, GROUP], U32, name="x_q", align_bytes=64) for g in range(GROUPS)]
        x_s = [ring.tile([P, GROUP], U8, name="x_s", align_bytes=64) for g in range(GROUPS)]
        x_bf = [ring.tile([P, GROUP, PACK], BF16, name="x_bf", align_bytes=64) for g in range(GROUPS)]
        tab_q = keep.tile([P, 2, 2 * J], U8, align_bytes=64)
        got_w = keep.tile([P, J], U32, align_bytes=64)
        h_bf = [ring.tile([P, w, PACK], BF16, name="h_bf", align_bytes=64) for w in WIDTHS[:-1]]
        h_bf += [over.tile([P, WIDTHS[-1], PACK], BF16, name="h_bf_last", align_bytes=64, offset=4096)]
        y_bf0 = over.tile([P, WIDTHS[0], PACK], BF16, align_bytes=64, offset=4096)
        h_q = [over.tile([P, w], U32, name="h_q1", align_bytes=64, offset=0) if c == 1 else ring.tile([P, w], U32, name="h_q", align_bytes=64) for c, w in enumerate(WIDTHS)]
        h_s = [ring.tile([P, w], U8, name="h_s", align_bytes=64) for w in WIDTHS]
        y_q = keep.tile([P, J], I32, align_bytes=64)
        act = [ring.tile([P, w, PACK], F32, name="act", align_bytes=64) for w in WIDTHS[:-1]]
        act += [over.tile([P, WIDTHS[-1], PACK], F32, name="act_last", align_bytes=64, offset=0)]
        yb_all = keep.tile([P, J // SUB, R], F32, align_bytes=64)
        yb_t = [yb_all[:, s, :] for s in range(J // SUB)]
        y_sb = keep.tile([P, PACK, J], F32, align_bytes=64)
        y_bf = over.tile([P, J, PACK], BF16, align_bytes=64, offset=4096)
        out_rows = out_0.rearrange("(p t) j -> p t j", t=PACK)

        def cols(c0, c1):
            return slice(STARTS[c0], STARTS[c1] + WIDTHS[c1])

        def quantize(codes, scales, src):
            nc.vector.quantize_mx(out=codes.bitcast(FP8X4), scales=scales, in_=src)

        def pick(i, place, g, n):
            tokens = slice(g * GROUP, (g + n) * GROUP)
            nc.vector.tensor_tensor(
                picks[:, place : place + n, :].rearrange("p s c -> p (s c)"),
                planes[i][:].indirect(idx2[:, tokens.start // 16 : tokens.stop // 16]), wgt[:, tokens], MULT,
            )

        def round_x(g):
            step = LATE[g] - g
            src = picks[:, g : g + 2 * step, :].rearrange("p (a x) c -> p a x c", a=2)[:, :, 0 : PACK + 1 : PACK, :]
            nc.scalar.copy(
                x_bf[g][:].rearrange("p (c i) (a e) -> p c a e i", i=4, a=2),
                src.rearrange("p a e (c i) -> p c a e i", i=4),
            )

        def quant_x(g):
            quantize(x_q[g][:], x_s[g][:], x_bf[g][:].rearrange("p c t -> p (c t)"))

        def deal_wd():
            nc.vector.tensor_copy(
                wd_q[:].rearrange("p (t m i) -> p m t i", t=PACK, i=4),
                wd_raw[:].rearrange("p (m i t) -> p m t i", t=PACK, i=4),
            )
            nc.vector.tensor_copy(
                wd_s[:].rearrange("p (t m) -> p t m", t=PACK), wd_s_raw[:].rearrange("p (m t) -> p t m", t=PACK)
            )

        def memory(s):
            yb = early[s % YB_BANKS]
            j0 = s * SUB
            for a in range(2):
                nc.tensor.matmul_mx(
                    out=yb[:], lhsT=tab_q[:, a, 2 * j0 : 2 * (j0 + SUB)].bitcast(FP4X4),
                    lhsT_scale=tab_planes[:, a, j0 : j0 + SUB],
                    rhs=wb_q[:, a, :].bitcast(FP4X4), rhs_scale=wb_s[:, a, :], start=(a == 0), stop=(a == 1),
                )
            nc.scalar.copy(yb_t[s].rearrange("p (t m) -> p t m", t=PACK), yb[:].rearrange("p (m t) -> p t m", t=PACK))

        def gate(g, blocks):
            for s in blocks:
                sub = slice(s * SUB, (s + 1) * SUB)
                ya = psum.tile([P, PACK, SUB], F32, name="bank")
                for t in range(PACK):
                    m = slice(t * P, (t + 1) * P)
                    nc.tensor.matmul_mx(
                        out=ya[:, t, :], lhsT=wa_q[:, m].bitcast(FP8X4), lhsT_scale=wa_s[:, m],
                        rhs=x_q[g][:, sub].bitcast(FP8X4), rhs_scale=x_s[g][:, sub], start=True, stop=True,
                    )
                dst = act[g][:, sub, :] if WIDTHS[g] == GROUP else act[g + s][:]
                nc.scalar.activation(dst, ya[:].rearrange("p t n -> p n t"), ACT.Silu)

        def join(c):
            for s in range(WIDTHS[c] // SUB):
                sub = slice(s * SUB, (s + 1) * SUB)
                yb = psum_yb.tile([P, PACK, SUB], F32, name="yb_bank")
                for t in range(PACK):
                    nc.tensor.transpose(yb[:, t, :], yb_t[STARTS[c] // SUB + s][:, t * P : (t + 1) * P], ident[:])
                nc.vector.tensor_tensor(h_bf[c][:, sub, :], act[c][:, sub, :], yb[:].rearrange("p t n -> p n t"), MULT)

        def quant_h(c):
            quantize(h_q[c][:], h_s[c][:], h_bf[c][:].rearrange("p c t -> p (c t)"))

        def project(out, t, c):
            m = slice(t * P, (t + 1) * P)
            nc.tensor.matmul_mx(
                out=out, lhsT=wd_q[:, m].bitcast(FP8X4), lhsT_scale=wd_s[:, m],
                rhs=h_q[c][:].bitcast(FP8X4), rhs_scale=h_s[c][:], start=True, stop=True,
            )

        def down(c):
            per_bank = BANK // WIDTHS[c]
            for t0 in range(0, PACK, per_bank):
                y = psum.tile([P, per_bank, WIDTHS[c]], F32, name="bank")
                for e in range(per_bank):
                    project(y[:, e, :], t0 + e, c)
                for e in range(per_bank):
                    t = t0 + e
                    nc.scalar.activation(y_sb[:, t, cols(c, c)], y[:, e, :], ACT.Identity, bias=bias[:, t : t + 1])
                rows = slice(t0, t0 + per_bank)
                if c:
                    nc.sync.dma_start(out_rows[:, rows, cols(c, c)], y_sb[:, rows, cols(c, c)])
            if c == 0:
                nc.sync.dma_start(out_rows[:, :, cols(c, c)], y_sb[:, :, cols(c, c)])

        def round_y(copy, c0, c1):
            copy(
                (y_bf if c0 else y_bf0)[:, cols(c0, c1), :].rearrange("p (c i) t -> p c t i", i=4),
                y_sb[:, :, cols(c0, c1)].rearrange("p t (c i) -> p c t i", i=4),
            )

        def round_from_sums(c):
            y = psum.tile([P, PACK, SUB], F32, name="bank")
            for t in range(PACK):
                project(y[:, t, :], t, c)
            nc.vector.tensor_tensor(
                y_bf[:, cols(c, c), :], y[:].rearrange("p t n -> p n t"),
                bias[:].unsqueeze(1).to_broadcast([P, SUB, PACK]), ADD,
            )

        def quant_y(c0, c1):
            quantize(y_q[:, cols(c0, c1)], out_s[:, cols(c0, c1)], (y_bf if c0 else y_bf0)[:, cols(c0, c1), :].rearrange("p c t -> p (c t)"))

        def store_codes(c0, c1):
            nc.sync.dma_start(out_1[0].rearrange("p j b -> p (j b)").bitcast(I32)[:, cols(c0, c1)], y_q[:, cols(c0, c1)])

        nc.vector.tensor_copy(got_w[:], tab_w[:].bitcast(U32).indirect(idx[:]))
        for u in range(2):
            half = slice(u * HALF, (u + 1) * HALF)
            nc.vector.tensor_copy(
                tab_q[:].bitcast(U16)[:, :, half], got_w[:, half].bitcast(U16).rearrange("p (j d) -> p d j", d=2)
            )
        wa_dealt = wa_bf[:].rearrange("p (t m i) -> p m i t", t=PACK, i=PACK)
        wa_half = [wa_raw[u][:].rearrange("p i (m t) -> p m i t", t=PACK) for u in range(2)]
        nc.scalar.copy(wa_dealt[:, 0 : P // 2], wa_half[0])
        nc.scalar.copy(wa_dealt[:, P // 2 : 3 * P // 4], wa_half[1][:, 0 : P // 4])
        nc.vector.tensor_copy(wa_dealt[:, 3 * P // 4 : P], wa_half[1][:, P // 4 : P // 2])
        quantize(wa_q[:], wa_s[:], wa_bf[:])
        early = [psum_yb.tile([P, R], F32, name="yb_bank") for e in range(YB_BANKS)]
        for s in range(J // SUB):
            memory(s)
        for i in range(2):
            pick(i, GROUPS * i, 0, GROUPS)
        pick(2, LATE[0], 0, GROUPS - 1)

        def chunks_of(g):
            return [c for c in range(CHUNKS) if STARTS[c] // GROUP == g]

        last = GROUPS - 1
        for k in range(GROUPS + 4):
            if k == last:
                pick(2, LATE[k], k, 1)
            if k <= last:
                pick(3, LATE[k] + PACK, k, 1)
                round_x(k)
            if k == 3:
                deal_wd()
            for c in chunks_of(k - 3):
                if c == CHUNKS - 1:
                    quant_h(c - 1)
                    round_y(nc.vector.tensor_copy, 0, 0)
                    quant_y(0, 0)
                    store_codes(0, 0)
                join(c)
            if 0 <= k - 1 <= last:
                quant_x(k - 1)
            for c in chunks_of(k - 3)[-1:]:
                quant_h(c)
            for c in chunks_of(k - 4):
                down(c)
            if 0 <= k - 1 <= last:
                gate(k - 1, range(GROUP // SUB if k <= last else 1))
            if k == last + 2:
                gate(last, [1])

        for c0, c1 in ((1, 1), (2, 3), (4, 4)):
            round_y(nc.scalar.copy if c0 == CHUNKS - 1 else nc.vector.tensor_copy, c0, c1)
            quant_y(c0, c1)
            store_codes(c0, c1)
        for r in range(4):
            queue = nc.scalar if r % 2 else nc.sync
            queue.dma_start(out_2[0, r:16:4, :].bitcast(I32), out_s[r:P:32, :].bitcast(I32))
